import numpy as np
import ml_dtypes


def mxq(x, axis, fmt="e4m3"):
    dtype, down = {"e4m3": (ml_dtypes.float8_e4m3fn, 7), "e5m2": (ml_dtypes.float8_e5m2, 14)}[fmt]
    v = np.moveaxis(np.asarray(x, np.float32).astype(ml_dtypes.bfloat16).astype(np.float64), axis, -1)
    blocks = v.reshape(v.shape[:-1] + (-1, 32))
    amax = np.abs(blocks).max(-1, keepdims=True)
    byte = np.maximum(np.where(amax > 0, np.frexp(amax)[1] - 1 + 127, 0) - down, 1)
    scale = np.exp2(byte - 127.0)
    codes = (blocks / scale).astype(np.float32).astype(dtype).astype(np.float64)
    return np.moveaxis((codes * scale).reshape(v.shape), -1, axis)


WIDE = False


def mx_kscale(k):
    if not WIDE:
        return np.ones(k)
    levels = np.array([10, -10, 5, -5, 0])
    if k % 512:
        return np.exp2(np.random.permutation(np.resize(levels, k // 32))).repeat(32)
    a = np.empty((k // 512, 16))
    for p in range(k // 512):
        a[p, :8] = np.random.permutation(np.resize(levels, 8))
        for g in range(8):
            far = levels[np.abs(levels - a[p, g]) >= 10]
            a[p, g + 8] = far[np.random.randint(len(far))]
    return np.exp2(a.ravel()).repeat(32)


def f64(x):
    return np.asarray(x).astype(np.float64)


def striped(idx):
    return np.tile(idx.reshape(-1, 16).T, (8, 1)).astype(np.uint16)


def unstriped(offs):
    return offs[:16].T.reshape(-1).astype(np.int64)


E2M1 = np.array([0.0, 0.5, 1.0, 1.5, 2.0, 3.0, 4.0, 6.0, -0.0, -0.5, -1.0, -1.5, -2.0, -3.0, -4.0, -6.0])


def pack_weight(w, fmt):
    k, n = w.shape
    w = f64(np.asarray(w, np.float32).astype(ml_dtypes.bfloat16)).reshape(k // 32, 32, n)
    amax = np.abs(w).max(1)
    if fmt == "e4m3":
        byte = np.frexp(amax)[1] - 1 + 127 - 7
    else:
        mant, ex = np.frexp(amax / 6.0)
        byte = np.where(mant > 0.5, ex, ex - 1) + 127
    byte = np.clip(np.where(amax > 0, byte, 1), 1, 254)
    scaled = (w * np.exp2(127.0 - byte)[:, None, :]).reshape(k, n).astype(np.float32)
    by_word = np.ascontiguousarray(scaled.reshape(k // 512, 128, 4, n).transpose(0, 1, 3, 2))
    if fmt == "e4m3":
        words = by_word.astype(ml_dtypes.float8_e4m3fn).view(np.uint8)
    else:
        c = by_word.astype(ml_dtypes.float4_e2m1fn).view(np.uint8) & 0xF
        words = (c[..., 0::2] | (c[..., 1::2] << 4)).reshape(k // 512, 128, 2 * n)
    return np.ascontiguousarray(words), np.ascontiguousarray(byte.astype(np.uint8).reshape(k // 512, 16, n))


def unpack_weight(words, scales, fmt):
    g, _, n = scales.shape
    words = np.ascontiguousarray(words).reshape(g, 128, n, -1)
    if fmt == "e4m3":
        vals = words.view(ml_dtypes.float8_e4m3fn).astype(np.float64)
    else:
        nib = np.empty((g, 128, n, 4), np.uint8)
        nib[..., 0::2] = words & 0xF
        nib[..., 1::2] = words >> 4
        vals = E2M1[nib]
    vals = vals * np.repeat(np.exp2(scales.astype(np.float64) - 127.0), 8, axis=1)[..., None]
    return vals.transpose(0, 1, 3, 2).reshape(g * 512, n)


def d_relu(v):
    return (v > 0).astype(np.float64)


K, T, G, C1, E, C2, H = 512, 768, 3, 256, 6, 128, 512
N = 512


def by_expert(wq, xq, E, C):
    return np.concatenate([wq[e].T @ xq[:, e * C:(e + 1) * C] for e in range(E)], axis=1)


def setup_inputs():
    n = np.random.standard_normal
    v = mx_kscale(N)
    u = mx_kscale(H)
    slots1 = np.random.permutation(T)
    slots2 = np.concatenate([q * C1 + np.random.permutation(C1) for q in range(G)])
    dy = pack_weight(n((N, T)) * v[:, None], "e4m3")
    return {
        "dy_words": dy[0],
        "dy_scales": dy[1],
        "wet": (n((E, N, H)) / np.sqrt(N) / v[None, :, None] * u).astype(np.float32),
        "wgt": (n((G, H, K)) / np.sqrt(H) / u[None, :, None]).astype(np.float32),
        "a": (n((H, T))).astype(np.float32),
        "gate": (np.tile(np.random.uniform(0.2, 1.0, T), (128, 1))).astype(np.float32),
        "offs": striped(slots1),
        "offs2": striped(slots2),
        "dst": striped(slots1[slots2]),
    }


def reference(dy_words, dy_scales, wet, wgt, a, gate, offs, offs2, dst):
    wetq = mxq(f64(wet), 1, "e4m3")
    wgtq = mxq(f64(wgt), 1, "e4m3")
    gq = unpack_weight(dy_words, dy_scales, "e4m3")[:, unstriped(dst)]
    z = f64(gate[:1]) * by_expert(wetq, gq, E, C2)
    da = np.zeros((H, T))
    da[:, unstriped(offs2)] = z
    dx = by_expert(wgtq, mxq(da * d_relu(f64(a)), 0, "e4m3"), G, C1)
    out = np.zeros((K, T))
    out[:, unstriped(offs)] = dx
    return out

@@ -1,0 +1,242 @@
+from contextlib import ExitStack
+
+import concourse.mybir as mybir
+
+F32 = mybir.dt.float32
+BF16 = mybir.dt.bfloat16
+I32 = mybir.dt.int32
+U32 = mybir.dt.uint32
+U16 = mybir.dt.uint16
+U8 = mybir.dt.uint8
+FP8X4 = mybir.dt.float8_e4m3fn_x4
+MULT = mybir.AluOpType.mult
+IS_GT = mybir.AluOpType.is_gt
+
+P = 128
+PACK = 4
+W = 512
+T = 768
+GROUPS = 3
+C1 = 256
+C2 = 128
+EXPERTS = 6
+PER_COL = 16
+
+FLOPS = 2 * 2 * W * W * T
+
+
+def tile_moe_hib_relu_kernel(
+    tc, dy_words, dy_scales, wet, wgt, a, gate, offs, offs2, dst, out
+):
+    nc = tc.nc
+    with ExitStack() as ctx:
+        lists = ctx.enter_context(tc.tile_pool(name="lists", bufs=1))
+        keep = ctx.enter_context(tc.tile_pool(name="keep", bufs=1))
+        psum = ctx.enter_context(tc.psum_pool(name="psum", bufs=8))
+
+        def sb(shape, dtype, name, tag=None):
+            return keep.tile(shape, dtype, name=name, tag=tag or name, align_bytes=64)
+
+        def load_list(src, name):
+            tile = lists.tile([P, T // PER_COL], U16, name=name)
+            nc.sync.dma_start(tile[:], src)
+            return tile
+
+        def entries(tile, first, count):
+            return tile[:, first // PER_COL : (first + count) // PER_COL]
+
+        def load_rows(src, first, count, name):
+            tile = sb([P, PACK, count], F32, name)
+            nc.sync.dma_start(
+                out=tile[:], in_=src.rearrange("(p j) c -> p j c", j=PACK)[:, :, first : first + count]
+            )
+            return tile
+
+        def load_gate(g):
+            tile = sb([P, C1], F32, "gate%d" % g)
+            nc.sync.dma_start(out=tile[:], in_=gate[:, g * C1 : (g + 1) * C1])
+            return tile
+
+        half = W // 2
+
+        dy_w = sb([P, T], U32, "dy_w")
+        dy_s = sb([P, T], U8, "dy_s")
+        nc.vector.memset(dy_s[:].bitcast(I32), 0)
+        nc.sync.dma_start(
+            out=dy_w[:].bitcast(I32), in_=dy_words[0].rearrange("p t d -> p (t d)").bitcast(I32)
+        )
+        scale_rows = dy_scales[0].bitcast(I32).rearrange("(q r) t -> r q t", r=PACK)
+        for r in range(PACK):
+            nc.sync.dma_start(out=dy_s[:].bitcast(I32)[r:P:32, :], in_=scale_rows[r])
+        dst_t = load_list(dst, "dst_t")
+        raw_e = {}
+        gates = {}
+        pre = {}
+        raw_g = {}
+        raw_e[0] = [load_rows(wet[0], h * half, half, "wet0_%d" % h) for h in range(2)]
+        raw_e[1] = [load_rows(wet[1], h * half, half, "wet1_%d" % h) for h in range(2)]
+        offs2_t = load_list(offs2, "offs2_t")
+        raw_e[2] = [load_rows(wet[2], 0, half, "wet2_0")]
+        gates[0] = load_gate(0)
+        raw_e[2].append(load_rows(wet[2], half, half, "wet2_1"))
+        raw_e[3] = [load_rows(wet[3], 0, W, "wet3")]
+        pre[0] = load_rows(a, 0, C1, "a0")
+        gates[1] = load_gate(1)
+        raw_e[4] = [load_rows(wet[4], 0, W, "wet4")]
+        raw_e[5] = [load_rows(wet[5], 0, W, "wet5")]
+        pre[1] = load_rows(a, C1, C1, "a1")
+        gates[2] = load_gate(2)
+        raw_g[0] = load_rows(wgt[0], 0, W, "wgt0")
+        pre[2] = load_rows(a, 2 * C1, C1, "a2")
+        offs_t = load_list(offs, "offs_t")
+        raw_g[1] = load_rows(wgt[1], 0, W, "wgt1")
+        raw_g[2] = load_rows(wgt[2], 0, W, "wgt2")
+
+        def copy_on(engine, out_ap, in_ap):
+            if engine == "vector":
+                nc.vector.tensor_copy(out=out_ap, in_=in_ap)
+            else:
+                nc.scalar.copy(out=out_ap, in_=in_ap)
+
+        def quantize(staged, words, name):
+            codes = sb([P, words], U32, name + "_codes")
+            scales = sb([P, words], U8, name + "_scales")
+            nc.vector.quantize_mx(out=codes[:].bitcast(FP8X4), scales=scales[:], in_=staged[:])
+            return codes, scales
+
+        def expert_weights(e):
+            staged = sb([P, W * PACK], BF16, "stage_e%d" % e)
+            view = staged[:].rearrange("p (t m j) -> p m t j", t=PACK, j=PACK)
+            pieces = raw_e[e]
+            m_count = P // len(pieces)
+            for h, raw in enumerate(pieces):
+                engine = "vector" if (e, h) == (1, 1) else "scalar"
+                copy_on(
+                    engine,
+                    view[:, h * m_count : (h + 1) * m_count],
+                    raw[:].rearrange("p j (m t) -> p m t j", t=PACK),
+                )
+            return quantize(staged, W, "we%d" % e)
+
+        def group_weights(g):
+            staged = sb([P, W * PACK], BF16, "stage_g%d" % g)
+            nc.scalar.copy(
+                out=staged[:].rearrange("p (c j) -> p c j", j=PACK),
+                in_=raw_g[g][:].rearrange("p j c -> p c j"),
+            )
+            return quantize(staged, W, "wg%d" % g)
+
+        def mm(acc, w, col, x_codes, x_scales):
+            cols = slice(col * P, (col + 1) * P)
+            nc.tensor.matmul_mx(
+                out=acc,
+                lhsT=w[0][:, cols].bitcast(FP8X4),
+                lhsT_scale=w[1][:, cols],
+                rhs=x_codes.bitcast(FP8X4),
+                rhs_scale=x_scales,
+                start=True,
+                stop=True,
+            )
+
+        g_w = sb([P, T], U32, "g_w")
+        g_s = sb([P, T], U8, "g_s")
+        for src, dest in ((dy_w, g_w), (dy_s, g_s)):
+            for first, count in ((0, C1), (C1, T - C1)):
+                nc.vector.tensor_copy(dest[:, first : first + count], src[:].indirect(entries(dst_t, first, count)))
+
+        we = {}
+        wg = {}
+        da_q = {}
+        mask_tag = {0: "stage_e3", 1: "stage_e5", 2: "stage_g0"}
+
+        def first_products(g):
+            z = sb([P, PACK, C1], F32, "z%d" % g)
+            if g == 0:
+                for x in range(2):
+                    bank = psum.tile([P, PACK, C2], F32, name="bank", tag="bank")
+                    slots = slice(x * C2, (x + 1) * C2)
+                    for r in range(PACK):
+                        mm(bank[:, r, :], we[x], r, g_w[:, slots], g_s[:, slots])
+                    nc.scalar.copy(out=z[:, :, slots], in_=bank[:])
+            else:
+                for h in range(2):
+                    bank = psum.tile([P, 2, C1], F32, name="bank", tag="bank")
+                    for x in range(2):
+                        e = 2 * g + x
+                        slots = slice(e * C2, (e + 1) * C2)
+                        for r in range(2):
+                            mm(bank[:, r, x * C2 : (x + 1) * C2], we[e], 2 * h + r, g_w[:, slots], g_s[:, slots])
+                    nc.scalar.copy(out=z[:, 2 * h : 2 * h + 2, :], in_=bank[:])
+            return z
+
+        def scatter_z(g, z):
+            wins = [sb([P, T], F32, "win%d_%d" % (g, r), tag="win%d" % r) for r in range(PACK)]
+            cuts = ((0, C2), (C2, C2)) if g == 0 else ((0, C1),)
+            for first, count in cuts:
+                for r in range(PACK):
+                    nc.vector.tensor_tensor(
+                        wins[r][:].indirect(entries(offs2_t, g * C1 + first, count)),
+                        z[:, r, first : first + count],
+                        gates[g][:, first : first + count],
+                        MULT,
+                    )
+            return wins
+
+        def masked(g, wins):
+            planes = sb([P, PACK, C1], BF16, "planes%d" % g, tag=mask_tag[g])
+            for r in range(PACK):
+                nc.vector.scalar_tensor_tensor(
+                    out=planes[:, r, :],
+                    in0=pre[g][:, r, :],
+                    scalar=0.0,
+                    in1=wins[r][:, g * C1 : (g + 1) * C1],
+                    op0=IS_GT,
+                    op1=MULT,
+                )
+            staged = sb([P, C1 * PACK], BF16, "stage_da%d" % g)
+            nc.scalar.copy(
+                out=staged[:].rearrange("p (c j) -> p c j", j=PACK),
+                in_=planes[:].rearrange("p j c -> p c j"),
+            )
+            return staged
+
+        def second_products(g, dx, col0):
+            for h in range(2):
+                bank = psum.tile([P, 2, C1], F32, name="bank", tag="bank")
+                for r in range(2):
+                    mm(bank[:, r, :], wg[g], 2 * h + r, da_q[g][0][:], da_q[g][1][:])
+                nc.scalar.copy(out=dx[:, 2 * h : 2 * h + 2, col0 : col0 + C1], in_=bank[:])
+
+        we[0] = expert_weights(0)
+        we[1] = expert_weights(1)
+        wins = scatter_z(0, first_products(0))
+        we[2] = expert_weights(2)
+        we[3] = expert_weights(3)
+        z = first_products(1)
+        staged = masked(0, wins)
+        wins = scatter_z(1, z)
+        da_q[0] = quantize(staged, C1, "da0")
+        we[4] = expert_weights(4)
+        we[5] = expert_weights(5)
+        z = first_products(2)
+        staged = masked(1, wins)
+        wins = scatter_z(2, z)
+        da_q[1] = quantize(staged, C1, "da1")
+        wg[0] = group_weights(0)
+        dx0 = sb([P, PACK, C1], F32, "dx0")
+        second_products(0, dx0, 0)
+        staged = masked(2, wins)
+        wg[1] = group_weights(1)
+        dx12 = sb([P, PACK, 2 * C1], F32, "dx12")
+        second_products(1, dx12, 0)
+        da_q[2] = quantize(staged, C1, "da2")
+        wg[2] = group_weights(2)
+        outs = [
+            sb([P, T], F32, "out%d" % r, tag=("win%d" % r if r < PACK - 1 else "stage_g2")) for r in range(PACK)
+        ]
+        for r in range(PACK):
+            nc.vector.tensor_copy(outs[r][:].indirect(entries(offs_t, 0, C1)), dx0[:, r, :])
+        second_products(2, dx12, C1)
+        for r in range(PACK):
+            nc.vector.tensor_copy(outs[r][:].indirect(entries(offs_t, C1, 2 * C1)), dx12[:, r, :])
+            nc.sync.dma_start(out=out[r * P : (r + 1) * P, :], in_=outs[r][:])

@@ -65,10 +65,10 @@ def tile_moe_hib_relu_kernel(
         nc.sync.dma_start(
             out=dy_w[:].bitcast(I32), in_=dy_words[0].rearrange("p t d -> p (t d)").bitcast(I32)
         )
+        dst_t = load_list(dst, "dst_t")
         scale_rows = dy_scales[0].bitcast(I32).rearrange("(q r) t -> r q t", r=PACK)
         for r in range(PACK):
             nc.sync.dma_start(out=dy_s[:].bitcast(I32)[r:P:32, :], in_=scale_rows[r])
-        dst_t = load_list(dst, "dst_t")
         raw_e = {}
         gates = {}
         pre = {}
@@ -80,17 +80,25 @@ def tile_moe_hib_relu_kernel(
         gates[0] = load_gate(0)
         raw_e[2].append(load_rows(wet[2], half, half, "wet2_1"))
         raw_e[3] = [load_rows(wet[3], 0, W, "wet3")]
+        raw_e[4] = [load_rows(wet[4], 0, half, "wet4_0")]
         pre[0] = load_rows(a, 0, C1, "a0")
         gates[1] = load_gate(1)
-        raw_e[4] = [load_rows(wet[4], 0, W, "wet4")]
+        raw_e[4].append(load_rows(wet[4], half, half, "wet4_1"))
         raw_e[5] = [load_rows(wet[5], 0, W, "wet5")]
+        raw_g[0] = [load_rows(wgt[0], 0, half, "wgt0_0")]
         pre[1] = load_rows(a, C1, C1, "a1")
         gates[2] = load_gate(2)
-        raw_g[0] = load_rows(wgt[0], 0, W, "wgt0")
+        raw_g[0].append(load_rows(wgt[0], half, half, "wgt0_1"))
         pre[2] = load_rows(a, 2 * C1, C1, "a2")
         offs_t = load_list(offs, "offs_t")
-        raw_g[1] = load_rows(wgt[1], 0, W, "wgt1")
-        raw_g[2] = load_rows(wgt[2], 0, W, "wgt2")
+        raw_g[1] = [load_rows(wgt[1], 0, W, "wgt1")]
+        raw_g[2] = [load_rows(wgt[2], 0, W, "wgt2")]
+
+        def weave(staged, rows):
+            nc.scalar.copy(
+                out=staged.rearrange("p (c i j) -> p c j i", i=PACK, j=PACK),
+                in_=rows.rearrange("p j (c i) -> p c j i", i=PACK),
+            )
 
         def copy_on(engine, out_ap, in_ap):
             if engine == "vector":
@@ -106,24 +114,24 @@ def tile_moe_hib_relu_kernel(
 
         def expert_weights(e):
             staged = sb([P, W * PACK], BF16, "stage_e%d" % e)
-            view = staged[:].rearrange("p (t m j) -> p m t j", t=PACK, j=PACK)
             pieces = raw_e[e]
             m_count = P // len(pieces)
             for h, raw in enumerate(pieces):
                 engine = "vector" if (e, h) == (1, 1) else "scalar"
+                order = "p m t j" if engine == "vector" else "p m j t"
+                view = staged[:].rearrange("p (t m j) -> " + order, t=PACK, j=PACK)
                 copy_on(
                     engine,
                     view[:, h * m_count : (h + 1) * m_count],
-                    raw[:].rearrange("p j (m t) -> p m t j", t=PACK),
+                    raw[:].rearrange("p j (m t) -> " + order, t=PACK),
                 )
             return quantize(staged, W, "we%d" % e)
 
         def group_weights(g):
             staged = sb([P, W * PACK], BF16, "stage_g%d" % g)
-            nc.scalar.copy(
-                out=staged[:].rearrange("p (c j) -> p c j", j=PACK),
-                in_=raw_g[g][:].rearrange("p j c -> p c j"),
-            )
+            width = W * PACK // len(raw_g[g])
+            for h, raw in enumerate(raw_g[g]):
+                weave(staged[:, h * width : (h + 1) * width], raw[:])
             return quantize(staged, W, "wg%d" % g)
 
         def mm(acc, w, col, x_codes, x_scales):
@@ -147,7 +155,7 @@ def tile_moe_hib_relu_kernel(
         we = {}
         wg = {}
         da_q = {}
-        mask_tag = {0: "stage_e3", 1: "stage_e5", 2: "stage_g0"}
+        mask_tag = {0: "stage_e3", 1: "stage_e5", 2: None}
 
         def first_products(g):
             z = sb([P, PACK, C1], F32, "z%d" % g)
@@ -170,7 +178,10 @@ def tile_moe_hib_relu_kernel(
             return z
 
         def scatter_z(g, z):
-            wins = [sb([P, T], F32, "win%d_%d" % (g, r), tag="win%d" % r) for r in range(PACK)]
+            tags = ["win%d" % r for r in range(PACK)]
+            if g == GROUPS - 1:
+                tags[-1] = "stage_g0"
+            wins = [sb([P, T], F32, "win%d_%d" % (g, r), tag=tags[r]) for r in range(PACK)]
             cuts = ((0, C2), (C2, C2)) if g == 0 else ((0, C1),)
             for first, count in cuts:
                 for r in range(PACK):
@@ -193,11 +204,11 @@ def tile_moe_hib_relu_kernel(
                     op0=IS_GT,
                     op1=MULT,
                 )
-            staged = sb([P, C1 * PACK], BF16, "stage_da%d" % g)
-            nc.scalar.copy(
-                out=staged[:].rearrange("p (c j) -> p c j", j=PACK),
-                in_=planes[:].rearrange("p j c -> p c j"),
-            )
+            return planes
+
+        def woven(g, planes):
+            staged = sb([P, C1 * PACK], BF16, "stage_da%d" % g, tag=("wet5" if g == 0 else None))
+            weave(staged[:], planes[:])
             return staged
 
         def second_products(g, dx, col0):
@@ -213,19 +224,20 @@ def tile_moe_hib_relu_kernel(
         we[2] = expert_weights(2)
         we[3] = expert_weights(3)
         z = first_products(1)
-        staged = masked(0, wins)
+        planes0 = masked(0, wins)
         wins = scatter_z(1, z)
-        da_q[0] = quantize(staged, C1, "da0")
         we[4] = expert_weights(4)
         we[5] = expert_weights(5)
+        staged0 = woven(0, planes0)
         z = first_products(2)
-        staged = masked(1, wins)
-        wins = scatter_z(2, z)
-        da_q[1] = quantize(staged, C1, "da1")
+        planes1 = masked(1, wins)
+        da_q[0] = quantize(staged0, C1, "da0")
         wg[0] = group_weights(0)
+        wins = scatter_z(2, z)
+        da_q[1] = quantize(woven(1, planes1), C1, "da1")
         dx0 = sb([P, PACK, C1], F32, "dx0")
         second_products(0, dx0, 0)
-        staged = masked(2, wins)
+        staged = woven(2, masked(2, wins))
         wg[1] = group_weights(1)
         dx12 = sb([P, PACK, 2 * C1], F32, "dx12")
         second_products(1, dx12, 0)

@@ -66,19 +66,18 @@ def tile_moe_hib_relu_kernel(
             out=dy_w[:].bitcast(I32), in_=dy_words[0].rearrange("p t d -> p (t d)").bitcast(I32)
         )
         dst_t = load_list(dst, "dst_t")
-        scale_rows = dy_scales[0].bitcast(I32).rearrange("(q r) t -> r q t", r=PACK)
-        for r in range(PACK):
-            nc.sync.dma_start(out=dy_s[:].bitcast(I32)[r:P:32, :], in_=scale_rows[r])
         raw_e = {}
         gates = {}
         pre = {}
         raw_g = {}
         raw_e[0] = [load_rows(wet[0], h * half, half, "wet0_%d" % h) for h in range(2)]
-        raw_e[1] = [load_rows(wet[1], h * half, half, "wet1_%d" % h) for h in range(2)]
+        scale_rows = dy_scales[0].bitcast(I32).rearrange("(q r) t -> r q t", r=PACK)
+        for r in range(PACK):
+            nc.sync.dma_start(out=dy_s[:].bitcast(I32)[r:P:32, :], in_=scale_rows[r])
         offs2_t = load_list(offs2, "offs2_t")
-        raw_e[2] = [load_rows(wet[2], 0, half, "wet2_0")]
         gates[0] = load_gate(0)
-        raw_e[2].append(load_rows(wet[2], half, half, "wet2_1"))
+        raw_e[1] = [load_rows(wet[1], h * half, half, "wet1_%d" % h) for h in range(2)]
+        raw_e[2] = [load_rows(wet[2], h * half, half, "wet2_%d" % h) for h in range(2)]
         raw_e[3] = [load_rows(wet[3], 0, W, "wet3")]
         raw_e[4] = [load_rows(wet[4], 0, half, "wet4_0")]
         pre[0] = load_rows(a, 0, C1, "a0")
@@ -86,9 +85,9 @@ def tile_moe_hib_relu_kernel(
         raw_e[4].append(load_rows(wet[4], half, half, "wet4_1"))
         raw_e[5] = [load_rows(wet[5], 0, W, "wet5")]
         raw_g[0] = [load_rows(wgt[0], 0, half, "wgt0_0")]
-        pre[1] = load_rows(a, C1, C1, "a1")
         gates[2] = load_gate(2)
         raw_g[0].append(load_rows(wgt[0], half, half, "wgt0_1"))
+        pre[1] = load_rows(a, C1, C1, "a1")
         pre[2] = load_rows(a, 2 * C1, C1, "a2")
         offs_t = load_list(offs, "offs_t")
         raw_g[1] = [load_rows(wgt[1], 0, W, "wgt1")]
@@ -117,7 +116,7 @@ def tile_moe_hib_relu_kernel(
             pieces = raw_e[e]
             m_count = P // len(pieces)
             for h, raw in enumerate(pieces):
-                engine = "vector" if (e, h) == (1, 1) else "scalar"
+                engine = "vector" if (e, h) == (0, 1) else "scalar"
                 order = "p m t j" if engine == "vector" else "p m j t"
                 view = staged[:].rearrange("p (t m j) -> " + order, t=PACK, j=PACK)
                 copy_on(
@@ -155,32 +154,31 @@ def tile_moe_hib_relu_kernel(
         we = {}
         wg = {}
         da_q = {}
-        mask_tag = {0: "stage_e3", 1: "stage_e5", 2: None}
+        mask_tag = {0: "stage_e3", 1: None, 2: None}
 
         def first_products(g):
             z = sb([P, PACK, C1], F32, "z%d" % g)
             if g == 0:
                 for x in range(2):
-                    bank = psum.tile([P, PACK, C2], F32, name="bank", tag="bank")
                     slots = slice(x * C2, (x + 1) * C2)
-                    for r in range(PACK):
-                        mm(bank[:, r, :], we[x], r, g_w[:, slots], g_s[:, slots])
-                    nc.scalar.copy(out=z[:, :, slots], in_=bank[:])
+                    for h in range(2):
+                        bank = psum.tile([P, 2, C2], F32, name="bank", tag="bank")
+                        for r in range(2):
+                            mm(bank[:, r, :], we[x], 2 * h + r, g_w[:, slots], g_s[:, slots])
+                        nc.scalar.copy(out=z[:, 2 * h : 2 * h + 2, slots], in_=bank[:])
             else:
-                for h in range(2):
-                    bank = psum.tile([P, 2, C1], F32, name="bank", tag="bank")
+                for r in range(PACK):
+                    bank = psum.tile([P, C1], F32, name="bank", tag="bank")
                     for x in range(2):
                         e = 2 * g + x
                         slots = slice(e * C2, (e + 1) * C2)
-                        for r in range(2):
-                            mm(bank[:, r, x * C2 : (x + 1) * C2], we[e], 2 * h + r, g_w[:, slots], g_s[:, slots])
-                    nc.scalar.copy(out=z[:, 2 * h : 2 * h + 2, :], in_=bank[:])
+                        mm(bank[:, x * C2 : (x + 1) * C2], we[e], r, g_w[:, slots], g_s[:, slots])
+                    nc.scalar.copy(out=z[:, r, :], in_=bank[:])
             return z
 
         def scatter_z(g, z):
             tags = ["win%d" % r for r in range(PACK)]
-            if g == GROUPS - 1:
-                tags[-1] = "stage_g0"
+            tags[-1] = "stage_g0" if g == GROUPS - 1 else "stage_e1"
             wins = [sb([P, T], F32, "win%d_%d" % (g, r), tag=tags[r]) for r in range(PACK)]
             cuts = ((0, C2), (C2, C2)) if g == 0 else ((0, C1),)
             for first, count in cuts:

@@ -11,6 +11,8 @@ U8 = mybir.dt.uint8
 FP8X4 = mybir.dt.float8_e4m3fn_x4
 MULT = mybir.AluOpType.mult
 IS_GT = mybir.AluOpType.is_gt
+SIGN = mybir.ActivationFunctionType.Sign
+RELU = mybir.ActivationFunctionType.Relu
 
 P = 128
 PACK = 4
@@ -105,8 +107,8 @@ def tile_moe_hib_relu_kernel(
             else:
                 nc.scalar.copy(out=out_ap, in_=in_ap)
 
-        def quantize(staged, words, name):
-            codes = sb([P, words], U32, name + "_codes")
+        def quantize(staged, words, name, tag=None):
+            codes = sb([P, words], U32, name + "_codes", tag=tag)
             scales = sb([P, words], U8, name + "_scales")
             nc.vector.quantize_mx(out=codes[:].bitcast(FP8X4), scales=scales[:], in_=staged[:])
             return codes, scales
@@ -126,12 +128,12 @@ def tile_moe_hib_relu_kernel(
                 )
             return quantize(staged, W, "we%d" % e)
 
-        def group_weights(g):
+        def group_weights(g, tag=None):
             staged = sb([P, W * PACK], BF16, "stage_g%d" % g)
             width = W * PACK // len(raw_g[g])
             for h, raw in enumerate(raw_g[g]):
                 weave(staged[:, h * width : (h + 1) * width], raw[:])
-            return quantize(staged, W, "wg%d" % g)
+            return quantize(staged, W, "wg%d" % g, tag)
 
         def mm(acc, w, col, x_codes, x_scales):
             cols = slice(col * P, (col + 1) * P)
@@ -178,7 +180,9 @@ def tile_moe_hib_relu_kernel(
 
         def scatter_z(g, z):
             tags = ["win%d" % r for r in range(PACK)]
-            tags[-1] = "stage_g0" if g == GROUPS - 1 else "stage_e1"
+            tags[-1] = "stage_e1"
+            if g == GROUPS - 1:
+                tags = tags[:2] + ["stage_g0", "stage_g1"]
             wins = [sb([P, T], F32, "win%d_%d" % (g, r), tag=tags[r]) for r in range(PACK)]
             cuts = ((0, C2), (C2, C2)) if g == 0 else ((0, C1),)
             for first, count in cuts:
@@ -231,22 +235,31 @@ def tile_moe_hib_relu_kernel(
         planes1 = masked(1, wins)
         da_q[0] = quantize(staged0, C1, "da0")
         wg[0] = group_weights(0)
-        wins = scatter_z(2, z)
         da_q[1] = quantize(woven(1, planes1), C1, "da1")
-        dx0 = sb([P, PACK, C1], F32, "dx0")
-        second_products(0, dx0, 0)
-        staged = woven(2, masked(2, wins))
         wg[1] = group_weights(1)
-        dx12 = sb([P, PACK, 2 * C1], F32, "dx12")
-        second_products(1, dx12, 0)
-        da_q[2] = quantize(staged, C1, "da2")
-        wg[2] = group_weights(2)
-        outs = [
-            sb([P, T], F32, "out%d" % r, tag=("win%d" % r if r < PACK - 1 else "stage_g2")) for r in range(PACK)
-        ]
+        wins = scatter_z(2, z)
+        dx01 = sb([P, PACK, 2 * C1], F32, "dx01")
+        second_products(0, dx01, 0)
+        second_products(1, dx01, C1)
+        signs = sb([P, PACK, C1], F32, "signs", tag="z0")
+        nc.scalar.activation(out=signs[:], in_=pre[2][:], func=SIGN)
+        mask = sb([P, PACK, C1], F32, "mask", tag="z1")
+        nc.scalar.activation(out=mask[:], in_=signs[:], func=RELU)
+        planes2 = sb([P, PACK, C1], F32, "planes2", tag="z2")
         for r in range(PACK):
-            nc.vector.tensor_copy(outs[r][:].indirect(entries(offs_t, 0, C1)), dx0[:, r, :])
-        second_products(2, dx12, C1)
+            nc.gpsimd.tensor_tensor(out=planes2[:, r, :], in0=wins[r][:, 2 * C1 : 3 * C1], in1=mask[:, r, :], op=MULT)
+        outs = [sb([P, T], F32, "out%d" % r) for r in range(PACK - 1)]
+        for g in range(2):
+            for r in range(PACK - 1):
+                nc.vector.tensor_copy(
+                    outs[r][:].indirect(entries(offs_t, g * C1, C1)), dx01[:, r, g * C1 : (g + 1) * C1]
+                )
+        da_q[2] = quantize(woven(2, planes2), C1, "da2")
+        wg[2] = group_weights(2, "z2")
+        dx2 = sb([P, PACK, C1], F32, "dx2")
+        second_products(2, dx2, 0)
+        outs.append(sb([P, T], F32, "out3", tag="stage_da2"))
+        nc.vector.tensor_copy(outs[3][:].indirect(entries(offs_t, 0, 2 * C1)), dx01[:, 3, :])
         for r in range(PACK):
-            nc.vector.tensor_copy(outs[r][:].indirect(entries(offs_t, C1, 2 * C1)), dx12[:, r, :])
+            nc.vector.tensor_copy(outs[r][:].indirect(entries(offs_t, 2 * C1, C1)), dx2[:, r, :])
             nc.sync.dma_start(out=out[r * P : (r + 1) * P, :], in_=outs[r][:])

@@ -10,9 +10,9 @@ U16 = mybir.dt.uint16
 U8 = mybir.dt.uint8
 FP8X4 = mybir.dt.float8_e4m3fn_x4
 MULT = mybir.AluOpType.mult
+ADD = mybir.AluOpType.add
 IS_GT = mybir.AluOpType.is_gt
-SIGN = mybir.ActivationFunctionType.Sign
-RELU = mybir.ActivationFunctionType.Relu
+COPY = mybir.ActivationFunctionType.Copy
 
 P = 128
 PACK = 4
@@ -34,7 +34,8 @@ def tile_moe_hib_relu_kernel(
     with ExitStack() as ctx:
         lists = ctx.enter_context(tc.tile_pool(name="lists", bufs=1))
         keep = ctx.enter_context(tc.tile_pool(name="keep", bufs=1))
-        psum = ctx.enter_context(tc.psum_pool(name="psum", bufs=8))
+        late = ctx.enter_context(tc.tile_pool(name="late", bufs=1))
+        psum = ctx.enter_context(tc.psum_pool(name="psum", bufs=1))
 
         def sb(shape, dtype, name, tag=None):
             return keep.tile(shape, dtype, name=name, tag=tag or name, align_bytes=64)
@@ -59,6 +60,45 @@ def tile_moe_hib_relu_kernel(
             nc.sync.dma_start(out=tile[:], in_=gate[:, g * C1 : (g + 1) * C1])
             return tile
 
+        def copy_on(engine, out_ap, in_ap):
+            if engine == "vector":
+                nc.vector.tensor_copy(out=out_ap, in_=in_ap)
+            elif engine == "gpsimd":
+                nc.gpsimd.tensor_scalar(out=out_ap, in0=in_ap, scalar1=1.0, scalar2=0.0, op0=MULT, op1=ADD)
+            else:
+                nc.scalar.copy(out=out_ap, in_=in_ap)
+
+        def scatter_on(engine, window, offsets, values):
+            if engine == "vector":
+                nc.vector.tensor_copy(window[:].indirect(offsets), values)
+            else:
+                nc.scalar.activation(window[:].indirect(offsets), values, COPY)
+
+        def weave(engine, staged, rows):
+            copy_on(
+                engine,
+                staged.rearrange("p (c i j) -> p c j i", i=PACK, j=PACK),
+                rows.rearrange("p j (c i) -> p c j i", i=PACK),
+            )
+
+        def quantize(staged, words, name):
+            codes = sb([P, words], U32, name + "_codes")
+            scales = sb([P, words], U8, name + "_scales")
+            nc.vector.quantize_mx(out=codes[:].bitcast(FP8X4), scales=scales[:], in_=staged)
+            return codes, scales
+
+        def mm(acc, w, col, x_codes, x_scales):
+            cols = slice(col * P, (col + 1) * P)
+            nc.tensor.matmul_mx(
+                out=acc,
+                lhsT=w[0][:, cols].bitcast(FP8X4),
+                lhsT_scale=w[1][:, cols],
+                rhs=x_codes.bitcast(FP8X4),
+                rhs_scale=x_scales,
+                start=True,
+                stop=True,
+            )
+
         half = W // 2
 
         dy_w = sb([P, T], U32, "dy_w")
@@ -76,76 +116,42 @@ def tile_moe_hib_relu_kernel(
         scale_rows = dy_scales[0].bitcast(I32).rearrange("(q r) t -> r q t", r=PACK)
         for r in range(PACK):
             nc.sync.dma_start(out=dy_s[:].bitcast(I32)[r:P:32, :], in_=scale_rows[r])
-        offs2_t = load_list(offs2, "offs2_t")
         gates[0] = load_gate(0)
+        offs2_t = load_list(offs2, "offs2_t")
         raw_e[1] = [load_rows(wet[1], h * half, half, "wet1_%d" % h) for h in range(2)]
-        raw_e[2] = [load_rows(wet[2], h * half, half, "wet2_%d" % h) for h in range(2)]
-        raw_e[3] = [load_rows(wet[3], 0, W, "wet3")]
-        raw_e[4] = [load_rows(wet[4], 0, half, "wet4_0")]
-        pre[0] = load_rows(a, 0, C1, "a0")
+        raw_e[2] = [load_rows(wet[2], 0, W, "wet2")]
         gates[1] = load_gate(1)
-        raw_e[4].append(load_rows(wet[4], half, half, "wet4_1"))
-        raw_e[5] = [load_rows(wet[5], 0, W, "wet5")]
-        raw_g[0] = [load_rows(wgt[0], 0, half, "wgt0_0")]
+        raw_e[3] = [load_rows(wet[3], 0, W, "wet3")]
+        raw_e[4] = [load_rows(wet[4], 0, W, "wet4")]
         gates[2] = load_gate(2)
-        raw_g[0].append(load_rows(wgt[0], half, half, "wgt0_1"))
-        pre[1] = load_rows(a, C1, C1, "a1")
-        pre[2] = load_rows(a, 2 * C1, C1, "a2")
+        raw_e[5] = [load_rows(wet[5], 0, W, "wet5")]
         offs_t = load_list(offs, "offs_t")
-        raw_g[1] = [load_rows(wgt[1], 0, W, "wgt1")]
-        raw_g[2] = [load_rows(wgt[2], 0, W, "wgt2")]
+        for g in range(GROUPS):
+            if g < GROUPS - 1:
+                pre[g] = load_rows(a, g * C1, C1, "a%d" % g)
+            raw_g[g] = load_rows(wgt[g], 0, W, "wgt%d" % g)
+        pre[GROUPS - 1] = load_rows(a, (GROUPS - 1) * C1, C1, "a%d" % (GROUPS - 1))
 
-        def weave(staged, rows):
-            nc.scalar.copy(
-                out=staged.rearrange("p (c i j) -> p c j i", i=PACK, j=PACK),
-                in_=rows.rearrange("p j (c i) -> p c j i", i=PACK),
-            )
+        ring = [sb([P, W * PACK], BF16, "stage%d" % s) for s in range(2)]
+        taken = []
 
-        def copy_on(engine, out_ap, in_ap):
-            if engine == "vector":
-                nc.vector.tensor_copy(out=out_ap, in_=in_ap)
-            else:
-                nc.scalar.copy(out=out_ap, in_=in_ap)
+        def stage(width):
+            taken.append(width)
+            return ring[len(taken) % 2][:, :width]
 
-        def quantize(staged, words, name, tag=None):
-            codes = sb([P, words], U32, name + "_codes", tag=tag)
-            scales = sb([P, words], U8, name + "_scales")
-            nc.vector.quantize_mx(out=codes[:].bitcast(FP8X4), scales=scales[:], in_=staged[:])
-            return codes, scales
-
-        def expert_weights(e):
-            staged = sb([P, W * PACK], BF16, "stage_e%d" % e)
+        def expert_weights(e, engines):
+            staged = stage(W * PACK)
             pieces = raw_e[e]
             m_count = P // len(pieces)
             for h, raw in enumerate(pieces):
-                engine = "vector" if (e, h) == (0, 1) else "scalar"
-                order = "p m t j" if engine == "vector" else "p m j t"
-                view = staged[:].rearrange("p (t m j) -> " + order, t=PACK, j=PACK)
+                order = "p m t j" if engines[h] == "vector" else "p m j t"
+                view = staged.rearrange("p (t m j) -> " + order, t=PACK, j=PACK)
                 copy_on(
-                    engine,
+                    engines[h],
                     view[:, h * m_count : (h + 1) * m_count],
                     raw[:].rearrange("p j (m t) -> " + order, t=PACK),
                 )
             return quantize(staged, W, "we%d" % e)
-
-        def group_weights(g, tag=None):
-            staged = sb([P, W * PACK], BF16, "stage_g%d" % g)
-            width = W * PACK // len(raw_g[g])
-            for h, raw in enumerate(raw_g[g]):
-                weave(staged[:, h * width : (h + 1) * width], raw[:])
-            return quantize(staged, W, "wg%d" % g, tag)
-
-        def mm(acc, w, col, x_codes, x_scales):
-            cols = slice(col * P, (col + 1) * P)
-            nc.tensor.matmul_mx(
-                out=acc,
-                lhsT=w[0][:, cols].bitcast(FP8X4),
-                lhsT_scale=w[1][:, cols],
-                rhs=x_codes.bitcast(FP8X4),
-                rhs_scale=x_scales,
-                start=True,
-                stop=True,
-            )
 
         g_w = sb([P, T], U32, "g_w")
         g_s = sb([P, T], U8, "g_s")
@@ -153,113 +159,85 @@ def tile_moe_hib_relu_kernel(
             for first, count in ((0, C1), (C1, T - C1)):
                 nc.vector.tensor_copy(dest[:, first : first + count], src[:].indirect(entries(dst_t, first, count)))
 
-        we = {}
+        conv = {0: ("scalar", "vector"), 1: ("scalar", "vector")}
+        wins = {}
+        for g in range(GROUPS):
+            z = None
+            wins[g] = [sb([P, (g + 1) * C1], F32, "win%d_%d" % (g, r)) for r in range(PACK)]
+            for x in range(2):
+                e = 2 * g + x
+                we = second if e == 1 else expert_weights(e, conv.get(e, ("vector",)))
+                slots = slice(e * C2, (e + 1) * C2)
+                bank = psum.tile([P, PACK, C2], F32, name="bank", tag="bank%d" % e)
+                for r in range(PACK):
+                    mm(bank[:, r, :], we, r, g_w[:, slots], g_s[:, slots])
+                own = slice(x * C2, (x + 1) * C2)
+                if x == 0:
+                    if g == 0:
+                        second = expert_weights(1, conv[1])
+                    z = sb([P, PACK, C1], F32, "z%d" % g, tag="wet1_0" if g == 0 else None)
+                nc.vector.tensor_tensor(
+                    out=z[:, :, own],
+                    in0=bank[:],
+                    in1=gates[g][:, own].unsqueeze(1).to_broadcast([P, PACK, C2]),
+                    op=MULT,
+                )
+                if g == 0:
+                    for r in range(PACK):
+                        scatter_on("scalar", wins[g][r], entries(offs2_t, e * C2, C2), z[:, r, own])
+            if g > 0:
+                for r in range(PACK):
+                    scatter_on("scalar", wins[g][r], entries(offs2_t, g * C1, C1), z[:, r, :])
+
+        dxs = {}
         wg = {}
         da_q = {}
-        mask_tag = {0: "stage_e3", 1: None, 2: None}
 
-        def first_products(g):
-            z = sb([P, PACK, C1], F32, "z%d" % g)
-            if g == 0:
-                for x in range(2):
-                    slots = slice(x * C2, (x + 1) * C2)
-                    for h in range(2):
-                        bank = psum.tile([P, 2, C2], F32, name="bank", tag="bank")
-                        for r in range(2):
-                            mm(bank[:, r, :], we[x], 2 * h + r, g_w[:, slots], g_s[:, slots])
-                        nc.scalar.copy(out=z[:, 2 * h : 2 * h + 2, slots], in_=bank[:])
-            else:
-                for r in range(PACK):
-                    bank = psum.tile([P, C1], F32, name="bank", tag="bank")
-                    for x in range(2):
-                        e = 2 * g + x
-                        slots = slice(e * C2, (e + 1) * C2)
-                        mm(bank[:, x * C2 : (x + 1) * C2], we[e], r, g_w[:, slots], g_s[:, slots])
-                    nc.scalar.copy(out=z[:, r, :], in_=bank[:])
-            return z
+        def group_weights(g):
+            staged = stage(W * PACK)
+            weave("vector", staged, raw_g[g][:])
+            wg[g] = quantize(staged, W, "wg%d" % g)
 
-        def scatter_z(g, z):
-            tags = ["win%d" % r for r in range(PACK)]
-            tags[-1] = "stage_e1"
-            if g == GROUPS - 1:
-                tags = tags[:2] + ["stage_g0", "stage_g1"]
-            wins = [sb([P, T], F32, "win%d_%d" % (g, r), tag=tags[r]) for r in range(PACK)]
-            cuts = ((0, C2), (C2, C2)) if g == 0 else ((0, C1),)
-            for first, count in cuts:
-                for r in range(PACK):
-                    nc.vector.tensor_tensor(
-                        wins[r][:].indirect(entries(offs2_t, g * C1 + first, count)),
-                        z[:, r, first : first + count],
-                        gates[g][:, first : first + count],
-                        MULT,
-                    )
-            return wins
-
-        def masked(g, wins):
-            planes = sb([P, PACK, C1], BF16, "planes%d" % g, tag=mask_tag[g])
+        def masked(g):
+            planes = stage(C1 * PACK).rearrange("p (r c) -> p r c", r=PACK)
             for r in range(PACK):
                 nc.vector.scalar_tensor_tensor(
                     out=planes[:, r, :],
                     in0=pre[g][:, r, :],
                     scalar=0.0,
-                    in1=wins[r][:, g * C1 : (g + 1) * C1],
+                    in1=wins[g][r][:, g * C1 : (g + 1) * C1],
                     op0=IS_GT,
                     op1=MULT,
                 )
-            return planes
+            if g < GROUPS - 1:
+                staged = stage(C1 * PACK)
+            else:
+                staged = late.tile([P, C1 * PACK], BF16, name="stage_last", offset=2048, align_bytes=64)[:]
+            weave("vector", staged, planes)
+            da_q[g] = quantize(staged, C1, "da%d" % g)
 
-        def woven(g, planes):
-            staged = sb([P, C1 * PACK], BF16, "stage_da%d" % g, tag=("wet5" if g == 0 else None))
-            weave(staged[:], planes[:])
-            return staged
-
-        def second_products(g, dx, col0):
+        def second_products(g):
+            dxs[g] = sb([P, PACK, C1], F32, "dx%d" % g)
             for h in range(2):
-                bank = psum.tile([P, 2, C1], F32, name="bank", tag="bank")
+                bank = psum.tile([P, 2, C1], F32, name="bank", tag="bank%d" % ((EXPERTS + 2 * g + h) % 8))
                 for r in range(2):
                     mm(bank[:, r, :], wg[g], 2 * h + r, da_q[g][0][:], da_q[g][1][:])
-                nc.scalar.copy(out=dx[:, 2 * h : 2 * h + 2, col0 : col0 + C1], in_=bank[:])
+                copy_on(("scalar", "vector")[h], dxs[g][:, 2 * h : 2 * h + 2, :], bank[:])
 
-        we[0] = expert_weights(0)
-        we[1] = expert_weights(1)
-        wins = scatter_z(0, first_products(0))
-        we[2] = expert_weights(2)
-        we[3] = expert_weights(3)
-        z = first_products(1)
-        planes0 = masked(0, wins)
-        wins = scatter_z(1, z)
-        we[4] = expert_weights(4)
-        we[5] = expert_weights(5)
-        staged0 = woven(0, planes0)
-        z = first_products(2)
-        planes1 = masked(1, wins)
-        da_q[0] = quantize(staged0, C1, "da0")
-        wg[0] = group_weights(0)
-        da_q[1] = quantize(woven(1, planes1), C1, "da1")
-        wg[1] = group_weights(1)
-        wins = scatter_z(2, z)
-        dx01 = sb([P, PACK, 2 * C1], F32, "dx01")
-        second_products(0, dx01, 0)
-        second_products(1, dx01, C1)
-        signs = sb([P, PACK, C1], F32, "signs", tag="z0")
-        nc.scalar.activation(out=signs[:], in_=pre[2][:], func=SIGN)
-        mask = sb([P, PACK, C1], F32, "mask", tag="z1")
-        nc.scalar.activation(out=mask[:], in_=signs[:], func=RELU)
-        planes2 = sb([P, PACK, C1], F32, "planes2", tag="z2")
+        masked(0)
+        group_weights(0)
+        second_products(0)
+        masked(1)
+        group_weights(1)
+        second_products(1)
+        group_weights(2)
+        masked(2)
+        second_products(2)
+        outs = [sb([P, T], F32, "out%d" % r) for r in range(2)]
+        for r in range(2):
+            outs.append(late.tile([P, T], F32, name="out%d" % (2 + r), offset=r * T * 4, align_bytes=64))
+        for g in range(GROUPS):
+            for r in range(PACK):
+                scatter_on("scalar" if r < 2 else "vector", outs[r], entries(offs_t, g * C1, C1), dxs[g][:, r, :])
         for r in range(PACK):
-            nc.gpsimd.tensor_tensor(out=planes2[:, r, :], in0=wins[r][:, 2 * C1 : 3 * C1], in1=mask[:, r, :], op=MULT)
-        outs = [sb([P, T], F32, "out%d" % r) for r in range(PACK - 1)]
-        for g in range(2):
-            for r in range(PACK - 1):
-                nc.vector.tensor_copy(
-                    outs[r][:].indirect(entries(offs_t, g * C1, C1)), dx01[:, r, g * C1 : (g + 1) * C1]
-                )
-        da_q[2] = quantize(woven(2, planes2), C1, "da2")
-        wg[2] = group_weights(2, "z2")
-        dx2 = sb([P, PACK, C1], F32, "dx2")
-        second_products(2, dx2, 0)
-        outs.append(sb([P, T], F32, "out3", tag="stage_da2"))
-        nc.vector.tensor_copy(outs[3][:].indirect(entries(offs_t, 0, 2 * C1)), dx01[:, 3, :])
-        for r in range(PACK):
-            nc.vector.tensor_copy(outs[r][:].indirect(entries(offs_t, 2 * C1, C1)), dx2[:, r, :])
             nc.sync.dma_start(out=out[r * P : (r + 1) * P, :], in_=outs[r][:])

@@ -103,22 +103,25 @@ def tile_moe_hib_relu_kernel(
 
         dy_w = sb([P, T], U32, "dy_w")
         dy_s = sb([P, T], U8, "dy_s")
-        nc.vector.memset(dy_s[:].bitcast(I32), 0)
+        dst_t = load_list(dst, "dst_t")
+        scale_rows = dy_scales[0].bitcast(I32)
+        for q in range(PACK):
+            nc.sync.dma_start(
+                out=dy_s[:].bitcast(I32)[32 * q : 32 * (q + 1), :],
+                in_=scale_rows[PACK * q : PACK * (q + 1), :].unsqueeze(0).to_broadcast([8, PACK, T // 4]),
+            )
         nc.sync.dma_start(
             out=dy_w[:].bitcast(I32), in_=dy_words[0].rearrange("p t d -> p (t d)").bitcast(I32)
         )
-        dst_t = load_list(dst, "dst_t")
         raw_e = {}
         gates = {}
         pre = {}
         raw_g = {}
         raw_e[0] = [load_rows(wet[0], h * half, half, "wet0_%d" % h) for h in range(2)]
-        scale_rows = dy_scales[0].bitcast(I32).rearrange("(q r) t -> r q t", r=PACK)
-        for r in range(PACK):
-            nc.sync.dma_start(out=dy_s[:].bitcast(I32)[r:P:32, :], in_=scale_rows[r])
+        raw_e[1] = [load_rows(wet[1], 0, half, "wet1_0")]
         gates[0] = load_gate(0)
         offs2_t = load_list(offs2, "offs2_t")
-        raw_e[1] = [load_rows(wet[1], h * half, half, "wet1_%d" % h) for h in range(2)]
+        raw_e[1].append(load_rows(wet[1], half, half, "wet1_1"))
         raw_e[2] = [load_rows(wet[2], 0, W, "wet2")]
         gates[1] = load_gate(1)
         raw_e[3] = [load_rows(wet[3], 0, W, "wet3")]
@@ -139,55 +142,52 @@ def tile_moe_hib_relu_kernel(
             taken.append(width)
             return ring[len(taken) % 2][:, :width]
 
-        def expert_weights(e, engines):
-            staged = stage(W * PACK)
-            pieces = raw_e[e]
-            m_count = P // len(pieces)
-            for h, raw in enumerate(pieces):
-                order = "p m t j" if engines[h] == "vector" else "p m j t"
-                view = staged.rearrange("p (t m j) -> " + order, t=PACK, j=PACK)
+        def expert_weights(e):
+            staged = sb([P, W * PACK], BF16, "stage_first")[:] if e == 0 else stage(W * PACK)
+            view = staged.rearrange("p (t m j) -> p m j t", t=PACK, j=PACK)
+            for h in range(2):
+                engine = "scalar" if (e < 2 and h == 0) else "vector"
                 copy_on(
-                    engines[h],
-                    view[:, h * m_count : (h + 1) * m_count],
-                    raw[:].rearrange("p j (m t) -> " + order, t=PACK),
+                    engine,
+                    view[:, h * P // 2 : (h + 1) * P // 2],
+                    raw_half(e, h).rearrange("p j (m t) -> p m j t", t=PACK),
                 )
             return quantize(staged, W, "we%d" % e)
 
-        g_w = sb([P, T], U32, "g_w")
-        g_s = sb([P, T], U8, "g_s")
-        for src, dest in ((dy_w, g_w), (dy_s, g_s)):
-            for first, count in ((0, C1), (C1, T - C1)):
-                nc.vector.tensor_copy(dest[:, first : first + count], src[:].indirect(entries(dst_t, first, count)))
+        def raw_half(e, h):
+            if len(raw_e[e]) == 2:
+                return raw_e[e][h][:]
+            return raw_e[e][0][:, :, h * half : (h + 1) * half]
 
-        conv = {0: ("scalar", "vector"), 1: ("scalar", "vector")}
-        wins = {}
-        for g in range(GROUPS):
-            z = None
-            wins[g] = [sb([P, (g + 1) * C1], F32, "win%d_%d" % (g, r)) for r in range(PACK)]
-            for x in range(2):
-                e = 2 * g + x
-                we = second if e == 1 else expert_weights(e, conv.get(e, ("vector",)))
-                slots = slice(e * C2, (e + 1) * C2)
-                bank = psum.tile([P, PACK, C2], F32, name="bank", tag="bank%d" % e)
-                for r in range(PACK):
-                    mm(bank[:, r, :], we, r, g_w[:, slots], g_s[:, slots])
-                own = slice(x * C2, (x + 1) * C2)
-                if x == 0:
-                    if g == 0:
-                        second = expert_weights(1, conv[1])
-                    z = sb([P, PACK, C1], F32, "z%d" % g, tag="wet1_0" if g == 0 else None)
-                nc.vector.tensor_tensor(
-                    out=z[:, :, own],
-                    in0=bank[:],
-                    in1=gates[g][:, own].unsqueeze(1).to_broadcast([P, PACK, C2]),
-                    op=MULT,
-                )
-                if g == 0:
-                    for r in range(PACK):
-                        scatter_on("scalar", wins[g][r], entries(offs2_t, e * C2, C2), z[:, r, own])
-            if g > 0:
-                for r in range(PACK):
-                    scatter_on("scalar", wins[g][r], entries(offs2_t, g * C1, C1), z[:, r, :])
+        g_w = sb([P, T], U32, "g_w")
+        for first, count in ((0, C1), (C1, T - C1)):
+            nc.vector.tensor_copy(g_w[:, first : first + count], dy_w[:].indirect(entries(dst_t, first, count)))
+        g_s0 = sb([P, C1], U8, "g_s0")
+        nc.vector.tensor_copy(g_s0[:], dy_s[:].indirect(entries(dst_t, 0, C1)))
+
+        wins = {g: [sb([P, (g + 1) * C1], F32, "win%d_%d" % (g, r)) for r in range(PACK)] for g in range(GROUPS)}
+        we = {0: expert_weights(0)}
+        g_s1 = sb([P, T - C1], U8, "g_s1", tag="stage_first")
+        nc.vector.tensor_copy(g_s1[:], dy_s[:].indirect(entries(dst_t, C1, T - C1)))
+        for e in range(EXPERTS):
+            g, x = divmod(e, 2)
+            slots = slice(e * C2, (e + 1) * C2)
+            bank = psum.tile([P, PACK, C2], F32, name="bank", tag="bank%d" % e)
+            for r in range(PACK):
+                mm(bank[:, r, :], we[e], r, g_w[:, slots], g_s0[:, slots] if g == 0 else g_s1[:, (e - 2) * C2 : (e - 1) * C2])
+            if e + 1 < EXPERTS:
+                we[e + 1] = expert_weights(e + 1)
+                z = raw_half(e + 1, 0)[:, :, :C2]
+            else:
+                z = sb([P, PACK, C2], F32, "z_last")[:]
+            nc.vector.tensor_tensor(
+                out=z,
+                in0=bank[:],
+                in1=gates[g][:, x * C2 : (x + 1) * C2].unsqueeze(1).to_broadcast([P, PACK, C2]),
+                op=MULT,
+            )
+            for r in range(PACK):
+                scatter_on("scalar", wins[g][r], entries(offs2_t, e * C2, C2), z[:, r, :])
 
         dxs = {}
         wg = {}
@@ -218,7 +218,7 @@ def tile_moe_hib_relu_kernel(
 
         def second_products(g):
             dxs[g] = sb([P, PACK, C1], F32, "dx%d" % g)
-            for h in range(2):
+            for h in (1, 0):
                 bank = psum.tile([P, 2, C1], F32, name="bank", tag="bank%d" % ((EXPERTS + 2 * g + h) % 8))
                 for r in range(2):
                     mm(bank[:, r, :], wg[g], 2 * h + r, da_q[g][0][:], da_q[g][1][:])
@@ -233,11 +233,11 @@ def tile_moe_hib_relu_kernel(
         group_weights(2)
         masked(2)
         second_products(2)
-        outs = [sb([P, T], F32, "out%d" % r) for r in range(2)]
-        for r in range(2):
-            outs.append(late.tile([P, T], F32, name="out%d" % (2 + r), offset=r * T * 4, align_bytes=64))
+        outs = [sb([P, T], F32, "out%d" % r) for r in range(PACK - 1)]
+        outs.append(late.tile([P, T], F32, name="out3", offset=0, align_bytes=64))
         for g in range(GROUPS):
-            for r in range(PACK):
-                scatter_on("scalar" if r < 2 else "vector", outs[r], entries(offs_t, g * C1, C1), dxs[g][:, r, :])
-        for r in range(PACK):
+            for r in (2, 0, 1, 3) if g < GROUPS - 1 else (0, 1, 3, 2):
+                engine = "vector" if r == 3 or (r == 2 and g == GROUPS - 1) else "scalar"
+                scatter_on(engine, outs[r], entries(offs_t, g * C1, C1), dxs[g][:, r, :])
+        for r in (3, 0, 2, 1):
             nc.sync.dma_start(out=out[r * P : (r + 1) * P, :], in_=outs[r][:])

@@ -34,7 +34,6 @@ def tile_moe_hib_relu_kernel(
     with ExitStack() as ctx:
         lists = ctx.enter_context(tc.tile_pool(name="lists", bufs=1))
         keep = ctx.enter_context(tc.tile_pool(name="keep", bufs=1))
-        late = ctx.enter_context(tc.tile_pool(name="late", bufs=1))
         psum = ctx.enter_context(tc.psum_pool(name="psum", bufs=1))
 
         def sb(shape, dtype, name, tag=None):
@@ -127,13 +126,13 @@ def tile_moe_hib_relu_kernel(
         raw_e[3] = [load_rows(wet[3], 0, W, "wet3")]
         raw_e[4] = [load_rows(wet[4], 0, W, "wet4")]
         gates[2] = load_gate(2)
+        pre[0] = load_rows(a, 0, C1, "a0")
         raw_e[5] = [load_rows(wet[5], 0, W, "wet5")]
         offs_t = load_list(offs, "offs_t")
         for g in range(GROUPS):
-            if g < GROUPS - 1:
-                pre[g] = load_rows(a, g * C1, C1, "a%d" % g)
             raw_g[g] = load_rows(wgt[g], 0, W, "wgt%d" % g)
-        pre[GROUPS - 1] = load_rows(a, (GROUPS - 1) * C1, C1, "a%d" % (GROUPS - 1))
+            if g > 0:
+                pre[g] = load_rows(a, g * C1, C1, "a%d" % g)
 
         ring = [sb([P, W * PACK], BF16, "stage%d" % s) for s in range(2)]
         taken = []
@@ -169,38 +168,38 @@ def tile_moe_hib_relu_kernel(
         we = {0: expert_weights(0)}
         g_s1 = sb([P, T - C1], U8, "g_s1", tag="stage_first")
         nc.vector.tensor_copy(g_s1[:], dy_s[:].indirect(entries(dst_t, C1, T - C1)))
-        for e in range(EXPERTS):
-            g, x = divmod(e, 2)
+        banks = {}
+
+        def first_products(e):
             slots = slice(e * C2, (e + 1) * C2)
-            bank = psum.tile([P, PACK, C2], F32, name="bank", tag="bank%d" % e)
+            banks[e] = psum.tile([P, PACK, C2], F32, name="bank", tag="bank%d" % e)
+            scales = g_s0[:, slots] if e < 2 else g_s1[:, (e - 2) * C2 : (e - 1) * C2]
             for r in range(PACK):
-                mm(bank[:, r, :], we[e], r, g_w[:, slots], g_s0[:, slots] if g == 0 else g_s1[:, (e - 2) * C2 : (e - 1) * C2])
-            if e + 1 < EXPERTS:
-                we[e + 1] = expert_weights(e + 1)
-                z = raw_half(e + 1, 0)[:, :, :C2]
-            else:
-                z = sb([P, PACK, C2], F32, "z_last")[:]
+                mm(banks[e][:, r, :], we[e], r, g_w[:, slots], scales)
+
+        def first_scatters(e, z):
+            g, x = divmod(e, 2)
             nc.vector.tensor_tensor(
                 out=z,
-                in0=bank[:],
+                in0=banks[e][:],
                 in1=gates[g][:, x * C2 : (x + 1) * C2].unsqueeze(1).to_broadcast([P, PACK, C2]),
                 op=MULT,
             )
             for r in range(PACK):
-                scatter_on("scalar", wins[g][r], entries(offs2_t, e * C2, C2), z[:, r, :])
+                engine = "vector" if (g, r) == (GROUPS - 1, PACK - 1) else "scalar"
+                scatter_on(engine, wins[g][r], entries(offs2_t, e * C2, C2), z[:, r, :])
 
-        dxs = {}
-        wg = {}
-        da_q = {}
+        for e in range(EXPERTS - 1):
+            first_products(e)
+            we[e + 1] = expert_weights(e + 1)
+            first_scatters(e, sb([P, PACK, C2], F32, "z0")[:] if e == 0 else raw_half(e + 1, 0)[:, :, :C2])
+        first_products(EXPERTS - 1)
 
-        def group_weights(g):
-            staged = stage(W * PACK)
-            weave("vector", staged, raw_g[g][:])
-            wg[g] = quantize(staged, W, "wg%d" % g)
+        dx = {}
+        outs = [sb([P, T], F32, "out%d" % r) for r in range(PACK - 1)]
 
-        def masked(g):
-            planes = stage(C1 * PACK).rearrange("p (r c) -> p r c", r=PACK)
-            for r in range(PACK):
+        def mask_planes(g, planes, rows):
+            for r in rows:
                 nc.vector.scalar_tensor_tensor(
                     out=planes[:, r, :],
                     in0=pre[g][:, r, :],
@@ -209,35 +208,41 @@ def tile_moe_hib_relu_kernel(
                     op0=IS_GT,
                     op1=MULT,
                 )
-            if g < GROUPS - 1:
-                staged = stage(C1 * PACK)
-            else:
-                staged = late.tile([P, C1 * PACK], BF16, name="stage_last", offset=2048, align_bytes=64)[:]
-            weave("vector", staged, planes)
-            da_q[g] = quantize(staged, C1, "da%d" % g)
 
-        def second_products(g):
-            dxs[g] = sb([P, PACK, C1], F32, "dx%d" % g)
-            for h in (1, 0):
-                bank = psum.tile([P, 2, C1], F32, name="bank", tag="bank%d" % ((EXPERTS + 2 * g + h) % 8))
-                for r in range(2):
-                    mm(bank[:, r, :], wg[g], 2 * h + r, da_q[g][0][:], da_q[g][1][:])
-                copy_on(("scalar", "vector")[h], dxs[g][:, 2 * h : 2 * h + 2, :], bank[:])
+        def empty(engine, g, h, dest):
+            copy_on(engine, dest, banks[g, h][:])
+            for r in range(2):
+                dx[g, 2 * h + r] = dest[:, r, :]
 
-        masked(0)
-        group_weights(0)
-        second_products(0)
-        masked(1)
-        group_weights(1)
-        second_products(1)
-        group_weights(2)
-        masked(2)
-        second_products(2)
-        outs = [sb([P, T], F32, "out%d" % r) for r in range(PACK - 1)]
-        outs.append(late.tile([P, T], F32, name="out3", offset=0, align_bytes=64))
+        def second_scatter(engine, g, r):
+            scatter_on(engine, outs[r], entries(offs_t, g * C1, C1), dx[g, r])
+
         for g in range(GROUPS):
-            for r in (2, 0, 1, 3) if g < GROUPS - 1 else (0, 1, 3, 2):
-                engine = "vector" if r == 3 or (r == 2 and g == GROUPS - 1) else "scalar"
-                scatter_on(engine, outs[r], entries(offs_t, g * C1, C1), dxs[g][:, r, :])
+            planes = sb([P, PACK, C1], BF16, "planes%d" % g)
+            mask_planes(g, planes, range(PACK))
+            if g > 0:
+                empty("vector", g - 1, 1, pre[g][:, 0:2, :])
+                second_scatter("scalar", g - 1, 2)
+            staged = sb([P, C1 * PACK], BF16, "stage_da%d" % g)
+            weave("vector", staged[:], planes[:])
+            da_q = quantize(staged[:], C1, "da%d" % g)
+            staged = sb([P, W * PACK], BF16, "stage_g%d" % g, tag="win%d_3" % g)
+            for h in range(2):
+                weave("vector", staged[:, h * W * 2 : (h + 1) * W * 2], raw_g[g][:, :, h * half : (h + 1) * half])
+            if g == 0:
+                first_scatters(EXPERTS - 1, raw_g[0][:, :, :C2])
+            wg = quantize(staged[:], W, "wg%d" % g)
+            for h in (1, 0):
+                banks[g, h] = psum.tile([P, 2, C1], F32, name="bank", tag="bank%d" % ((EXPERTS + 2 * g + h) % 8))
+                for r in range(2):
+                    mm(banks[g, h][:, r, :], wg, 2 * h + r, da_q[0][:], da_q[1][:])
+            empty("scalar", g, 0, sb([P, 2, C1], F32, "dx%d" % g)[:])
+            for r in range(2):
+                second_scatter("scalar", g, r)
+        outs.append(sb([P, T], F32, "out3", tag="win2_3"))
+        second_scatter("vector", 0, 3)
+        empty("vector", 2, 1, sb([P, 2, C1], F32, "dx_last")[:])
+        for g, r in ((1, 3), (2, 3), (2, 2)):
+            second_scatter("vector", g, r)
         for r in (3, 0, 2, 1):
             nc.sync.dma_start(out=out[r * P : (r + 1) * P, :], in_=outs[r][:])

@@ -126,8 +126,8 @@ def tile_moe_hib_relu_kernel(
         raw_e[3] = [load_rows(wet[3], 0, W, "wet3")]
         raw_e[4] = [load_rows(wet[4], 0, W, "wet4")]
         gates[2] = load_gate(2)
-        pre[0] = load_rows(a, 0, C1, "a0")
         raw_e[5] = [load_rows(wet[5], 0, W, "wet5")]
+        pre[0] = load_rows(a, 0, C1, "a0")
         offs_t = load_list(offs, "offs_t")
         for g in range(GROUPS):
             raw_g[g] = load_rows(wgt[g], 0, W, "wgt%d" % g)
@@ -214,8 +214,8 @@ def tile_moe_hib_relu_kernel(
             for r in range(2):
                 dx[g, 2 * h + r] = dest[:, r, :]
 
-        def second_scatter(engine, g, r):
-            scatter_on(engine, outs[r], entries(offs_t, g * C1, C1), dx[g, r])
+        def second_scatter(engine, g, r, first=0, count=C1):
+            scatter_on(engine, outs[r], entries(offs_t, g * C1 + first, count), dx[g, r][:, first : first + count])
 
         for g in range(GROUPS):
             planes = sb([P, PACK, C1], BF16, "planes%d" % g)
@@ -223,14 +223,14 @@ def tile_moe_hib_relu_kernel(
             if g > 0:
                 empty("vector", g - 1, 1, pre[g][:, 0:2, :])
                 second_scatter("scalar", g - 1, 2)
+            else:
+                first_scatters(EXPERTS - 1, pre[g][:, 0:2, :].rearrange("p a (b c) -> p (a b) c", b=2))
             staged = sb([P, C1 * PACK], BF16, "stage_da%d" % g)
             weave("vector", staged[:], planes[:])
             da_q = quantize(staged[:], C1, "da%d" % g)
             staged = sb([P, W * PACK], BF16, "stage_g%d" % g, tag="win%d_3" % g)
             for h in range(2):
                 weave("vector", staged[:, h * W * 2 : (h + 1) * W * 2], raw_g[g][:, :, h * half : (h + 1) * half])
-            if g == 0:
-                first_scatters(EXPERTS - 1, raw_g[0][:, :, :C2])
             wg = quantize(staged[:], W, "wg%d" % g)
             for h in (1, 0):
                 banks[g, h] = psum.tile([P, 2, C1], F32, name="bank", tag="bank%d" % ((EXPERTS + 2 * g + h) % 8))
@@ -242,7 +242,9 @@ def tile_moe_hib_relu_kernel(
         outs.append(sb([P, T], F32, "out3", tag="win2_3"))
         second_scatter("vector", 0, 3)
         empty("vector", 2, 1, sb([P, 2, C1], F32, "dx_last")[:])
-        for g, r in ((1, 3), (2, 3), (2, 2)):
+        for g, r in ((1, 3), (2, 3)):
             second_scatter("vector", g, r)
-        for r in (3, 0, 2, 1):
+        second_scatter("vector", 2, 2, 0, C2)
+        second_scatter("scalar", 2, 2, C2, C2)
+        for r in (3, 0, 1, 2):
             nc.sync.dma_start(out=out[r * P : (r + 1) * P, :], in_=outs[r][:])

@@ -23,6 +23,7 @@ C1 = 256
 C2 = 128
 EXPERTS = 6
 PER_COL = 16
+SCALAR_WORDS = 44
 
 FLOPS = 2 * 2 * W * W * T
 
@@ -116,7 +117,7 @@ def tile_moe_hib_relu_kernel(
         gates = {}
         pre = {}
         raw_g = {}
-        raw_e[0] = [load_rows(wet[0], h * half, half, "wet0_%d" % h) for h in range(2)]
+        raw_e[0] = [load_rows(wet[0], 0, W, "wet0")]
         raw_e[1] = [load_rows(wet[1], 0, half, "wet1_0")]
         gates[0] = load_gate(0)
         offs2_t = load_list(offs2, "offs2_t")
@@ -144,12 +145,13 @@ def tile_moe_hib_relu_kernel(
         def expert_weights(e):
             staged = sb([P, W * PACK], BF16, "stage_first")[:] if e == 0 else stage(W * PACK)
             view = staged.rearrange("p (t m j) -> p m j t", t=PACK, j=PACK)
-            for h in range(2):
-                engine = "scalar" if (e < 2 and h == 0) else "vector"
+            cut = SCALAR_WORDS if e == 0 else P // 2
+            for h, (first, last) in enumerate(((0, cut), (cut, P))):
+                rows = raw_e[e][0][:, :, PACK * first : PACK * last] if e == 0 else raw_half(e, h)
                 copy_on(
-                    engine,
-                    view[:, h * P // 2 : (h + 1) * P // 2],
-                    raw_half(e, h).rearrange("p j (m t) -> p m j t", t=PACK),
+                    "scalar" if (e < 2 and h == 0) else "vector",
+                    view[:, first:last],
+                    rows.rearrange("p j (m t) -> p m j t", t=PACK),
                 )
             return quantize(staged, W, "we%d" % e)
 
@@ -161,19 +163,20 @@ def tile_moe_hib_relu_kernel(
         g_w = sb([P, T], U32, "g_w")
         for first, count in ((0, C1), (C1, T - C1)):
             nc.vector.tensor_copy(g_w[:, first : first + count], dy_w[:].indirect(entries(dst_t, first, count)))
-        g_s0 = sb([P, C1], U8, "g_s0")
-        nc.vector.tensor_copy(g_s0[:], dy_s[:].indirect(entries(dst_t, 0, C1)))
+        g_s0 = sb([P, 2 * C1], U8, "g_s0")
+        for first in (0, C1):
+            nc.vector.tensor_copy(g_s0[:, first : first + C1], dy_s[:].indirect(entries(dst_t, first, C1)))
 
         wins = {g: [sb([P, (g + 1) * C1], F32, "win%d_%d" % (g, r)) for r in range(PACK)] for g in range(GROUPS)}
         we = {0: expert_weights(0)}
-        g_s1 = sb([P, T - C1], U8, "g_s1", tag="stage_first")
-        nc.vector.tensor_copy(g_s1[:], dy_s[:].indirect(entries(dst_t, C1, T - C1)))
+        g_s1 = sb([P, C1], U8, "g_s1", tag="stage_first")
+        nc.vector.tensor_copy(g_s1[:], dy_s[:].indirect(entries(dst_t, 2 * C1, C1)))
         banks = {}
 
         def first_products(e):
             slots = slice(e * C2, (e + 1) * C2)
             banks[e] = psum.tile([P, PACK, C2], F32, name="bank", tag="bank%d" % e)
-            scales = g_s0[:, slots] if e < 2 else g_s1[:, (e - 2) * C2 : (e - 1) * C2]
+            scales = g_s0[:, slots] if e < 4 else g_s1[:, (e - 4) * C2 : (e - 3) * C2]
             for r in range(PACK):
                 mm(banks[e][:, r, :], we[e], r, g_w[:, slots], scales)
 
@@ -186,7 +189,7 @@ def tile_moe_hib_relu_kernel(
                 op=MULT,
             )
             for r in range(PACK):
-                engine = "vector" if (g, r) == (GROUPS - 1, PACK - 1) else "scalar"
+                engine = "vector" if (g, r) == (1, PACK - 1) else "scalar"
                 scatter_on(engine, wins[g][r], entries(offs2_t, e * C2, C2), z[:, r, :])
 
         for e in range(EXPERTS - 1):

@@ -23,6 +23,7 @@ C1 = 256
 C2 = 128
 EXPERTS = 6
 PER_COL = 16
+VECTOR_SHARE = 160
 SCALAR_WORDS = 44
 
 FLOPS = 2 * 2 * W * W * T
@@ -123,11 +124,11 @@ def tile_moe_hib_relu_kernel(
         offs2_t = load_list(offs2, "offs2_t")
         raw_e[1].append(load_rows(wet[1], half, half, "wet1_1"))
         raw_e[2] = [load_rows(wet[2], 0, W, "wet2")]
-        gates[1] = load_gate(1)
         raw_e[3] = [load_rows(wet[3], 0, W, "wet3")]
+        gates[1] = load_gate(1)
         raw_e[4] = [load_rows(wet[4], 0, W, "wet4")]
-        gates[2] = load_gate(2)
         raw_e[5] = [load_rows(wet[5], 0, W, "wet5")]
+        gates[2] = load_gate(2)
         pre[0] = load_rows(a, 0, C1, "a0")
         offs_t = load_list(offs, "offs_t")
         for g in range(GROUPS):
@@ -213,8 +214,11 @@ def tile_moe_hib_relu_kernel(
                 )
 
         def empty(engine, g, h, dest):
-            copy_on(engine, dest, banks[g, h][:])
+            if engine == "vector":
+                copy_on(engine, dest, banks[g, h][:])
             for r in range(2):
+                if engine == "scalar":
+                    copy_on(engine, dest[:, r, :], banks[g, h][:, r, :])
                 dx[g, 2 * h + r] = dest[:, r, :]
 
         def second_scatter(engine, g, r, first=0, count=C1):
@@ -232,8 +236,7 @@ def tile_moe_hib_relu_kernel(
             weave("vector", staged[:], planes[:])
             da_q = quantize(staged[:], C1, "da%d" % g)
             staged = sb([P, W * PACK], BF16, "stage_g%d" % g, tag="win%d_3" % g)
-            for h in range(2):
-                weave("vector", staged[:, h * W * 2 : (h + 1) * W * 2], raw_g[g][:, :, h * half : (h + 1) * half])
+            weave("vector", staged[:], raw_g[g][:])
             wg = quantize(staged[:], W, "wg%d" % g)
             for h in (1, 0):
                 banks[g, h] = psum.tile([P, 2, C1], F32, name="bank", tag="bank%d" % ((EXPERTS + 2 * g + h) % 8))
@@ -243,11 +246,10 @@ def tile_moe_hib_relu_kernel(
             for r in range(2):
                 second_scatter("scalar", g, r)
         outs.append(sb([P, T], F32, "out3", tag="win2_3"))
-        second_scatter("vector", 0, 3)
+        second_scatter("vector", 0, 3, 0, VECTOR_SHARE)
         empty("vector", 2, 1, sb([P, 2, C1], F32, "dx_last")[:])
-        for g, r in ((1, 3), (2, 3)):
+        for g, r in ((1, 3), (2, 2), (2, 3)):
             second_scatter("vector", g, r)
-        second_scatter("vector", 2, 2, 0, C2)
-        second_scatter("scalar", 2, 2, C2, C2)
-        for r in (3, 0, 1, 2):
+        second_scatter("scalar", 0, 3, VECTOR_SHARE, C1 - VECTOR_SHARE)
+        for r in (2, 0, 1, 3):
             nc.sync.dma_start(out=out[r * P : (r + 1) * P, :], in_=outs[r][:])

@@ -23,7 +23,7 @@ C1 = 256
 C2 = 128
 EXPERTS = 6
 PER_COL = 16
-VECTOR_SHARE = 160
+OWN = 128
 SCALAR_WORDS = 44
 
 FLOPS = 2 * 2 * W * W * T
@@ -224,20 +224,9 @@ def tile_moe_hib_relu_kernel(
         def second_scatter(engine, g, r, first=0, count=C1):
             scatter_on(engine, outs[r], entries(offs_t, g * C1 + first, count), dx[g, r][:, first : first + count])
 
-        for g in range(GROUPS):
-            planes = sb([P, PACK, C1], BF16, "planes%d" % g)
-            mask_planes(g, planes, range(PACK))
-            if g > 0:
-                empty("vector", g - 1, 1, pre[g][:, 0:2, :])
-                second_scatter("scalar", g - 1, 2)
-            else:
-                first_scatters(EXPERTS - 1, pre[g][:, 0:2, :].rearrange("p a (b c) -> p (a b) c", b=2))
-            staged = sb([P, C1 * PACK], BF16, "stage_da%d" % g)
-            weave("vector", staged[:], planes[:])
-            da_q = quantize(staged[:], C1, "da%d" % g)
-            staged = sb([P, W * PACK], BF16, "stage_g%d" % g, tag="win%d_3" % g)
-            weave("vector", staged[:], raw_g[g][:])
-            wg = quantize(staged[:], W, "wg%d" % g)
+        outs.append(sb([P, T], F32, "out3"))
+
+        def products(g, wg, da_q):
             for h in (1, 0):
                 banks[g, h] = psum.tile([P, 2, C1], F32, name="bank", tag="bank%d" % ((EXPERTS + 2 * g + h) % 8))
                 for r in range(2):
@@ -245,11 +234,46 @@ def tile_moe_hib_relu_kernel(
             empty("scalar", g, 0, sb([P, 2, C1], F32, "dx%d" % g)[:])
             for r in range(2):
                 second_scatter("scalar", g, r)
-        outs.append(sb([P, T], F32, "out3", tag="win2_3"))
-        second_scatter("vector", 0, 3, 0, VECTOR_SHARE)
-        empty("vector", 2, 1, sb([P, 2, C1], F32, "dx_last")[:])
-        for g, r in ((1, 3), (2, 2), (2, 3)):
-            second_scatter("vector", g, r)
-        second_scatter("scalar", 0, 3, VECTOR_SHARE, C1 - VECTOR_SHARE)
-        for r in (2, 0, 1, 3):
+
+        def empty_high(g, dest):
+            for r in (1, 0):
+                copy_on("vector", dest[:, r, :], banks[g, 1][:, r, :])
+                dx[g, 2 + r] = dest[:, r, :]
+
+        for g in range(GROUPS):
+            planes = sb([P, PACK, C1], BF16, "planes%d" % g)
+            mask_planes(g, planes, range(PACK))
+            if g == 0:
+                first_scatters(EXPERTS - 1, pre[g][:, 0:2, :].rearrange("p a (b c) -> p (a b) c", b=2))
+                staged = sb([P, C1 * PACK], BF16, "stage_da%d" % g)
+                weave("vector", staged[:], planes[:])
+                da_q = quantize(staged[:], C1, "da%d" % g)
+                staged = sb([P, W * PACK], BF16, "stage_g%d" % g, tag="win%d_3" % g)
+                weave("vector", staged[:], raw_g[g][:])
+                wg = quantize(staged[:], W, "wg%d" % g)
+            else:
+                codes = sb([P, W], U32, "wg%d_codes" % g)
+                scales = sb([P, W], U8, "wg%d_scales" % g)
+                wg = (codes, scales)
+                own = sb([P, OWN * PACK], BF16, "stage_own%d" % g, tag="win%d_1" % g)
+                weave("vector", own[:], raw_g[g][:, :, :OWN])
+                staged = sb([P, C1 * PACK], BF16, "stage_da%d" % g)
+                weave("vector", staged[:], planes[:])
+                nc.vector.quantize_mx(out=codes[:, :OWN].bitcast(FP8X4), scales=scales[:, :OWN], in_=own[:])
+                da_q = quantize(staged[:], C1, "da%d" % g)
+                lent = sb([P, (W - OWN) * PACK], BF16, "stage_lent%d" % g, tag="stage_da%d" % g)
+                copy_on(
+                    "gpsimd",
+                    lent[:].rearrange("p (c j) -> p c j", j=PACK),
+                    raw_g[g][:, :, OWN:].rearrange("p j c -> p c j"),
+                )
+                empty_high(g - 1, sb([P, 2, C1], F32, "dx_high%d" % g, tag="planes%d" % g)[:])
+                second_scatter("vector", g - 1, 3)
+                second_scatter("scalar", g - 1, 2)
+                nc.vector.quantize_mx(out=codes[:, OWN:].bitcast(FP8X4), scales=scales[:, OWN:], in_=lent[:])
+            products(g, wg, da_q)
+        empty_high(2, sb([P, 2, C1], F32, "dx_last")[:])
+        for r in (3, 2):
+            second_scatter("vector", 2, r)
+        for r in (3, 0, 2, 1):
             nc.sync.dma_start(out=out[r * P : (r + 1) * P, :], in_=outs[r][:])

@@ -23,7 +23,7 @@ C1 = 256
 C2 = 128
 EXPERTS = 6
 PER_COL = 16
-OWN = 128
+LENT = 384
 SCALAR_WORDS = 44
 
 FLOPS = 2 * 2 * W * W * T
@@ -119,10 +119,9 @@ def tile_moe_hib_relu_kernel(
         pre = {}
         raw_g = {}
         raw_e[0] = [load_rows(wet[0], 0, W, "wet0")]
-        raw_e[1] = [load_rows(wet[1], 0, half, "wet1_0")]
         gates[0] = load_gate(0)
         offs2_t = load_list(offs2, "offs2_t")
-        raw_e[1].append(load_rows(wet[1], half, half, "wet1_1"))
+        raw_e[1] = [load_rows(wet[1], 0, W, "wet1")]
         raw_e[2] = [load_rows(wet[2], 0, W, "wet2")]
         raw_e[3] = [load_rows(wet[3], 0, W, "wet3")]
         gates[1] = load_gate(1)
@@ -130,11 +129,14 @@ def tile_moe_hib_relu_kernel(
         raw_e[5] = [load_rows(wet[5], 0, W, "wet5")]
         gates[2] = load_gate(2)
         pre[0] = load_rows(a, 0, C1, "a0")
+        raw_own = {0: load_rows(wgt[0], LENT, W - LENT, "wgt0_own")[:]}
         offs_t = load_list(offs, "offs_t")
-        for g in range(GROUPS):
+        raw_lent = {0: load_rows(wgt[0], 0, LENT, "wgt0")[:]}
+        for g in range(1, GROUPS):
             raw_g[g] = load_rows(wgt[g], 0, W, "wgt%d" % g)
-            if g > 0:
-                pre[g] = load_rows(a, g * C1, C1, "a%d" % g)
+            raw_own[g] = raw_g[g][:, :, LENT:]
+            raw_lent[g] = raw_g[g][:, :, :LENT]
+            pre[g] = load_rows(a, g * C1, C1, "a%d" % g)
 
         ring = [sb([P, W * PACK], BF16, "stage%d" % s) for s in range(2)]
         taken = []
@@ -146,9 +148,9 @@ def tile_moe_hib_relu_kernel(
         def expert_weights(e):
             staged = sb([P, W * PACK], BF16, "stage_first")[:] if e == 0 else stage(W * PACK)
             view = staged.rearrange("p (t m j) -> p m j t", t=PACK, j=PACK)
-            cut = SCALAR_WORDS if e == 0 else P // 2
+            cut = SCALAR_WORDS if e < 2 else P // 2
             for h, (first, last) in enumerate(((0, cut), (cut, P))):
-                rows = raw_e[e][0][:, :, PACK * first : PACK * last] if e == 0 else raw_half(e, h)
+                rows = raw_e[e][0][:, :, PACK * first : PACK * last]
                 copy_on(
                     "scalar" if (e < 2 and h == 0) else "vector",
                     view[:, first:last],
@@ -157,8 +159,6 @@ def tile_moe_hib_relu_kernel(
             return quantize(staged, W, "we%d" % e)
 
         def raw_half(e, h):
-            if len(raw_e[e]) == 2:
-                return raw_e[e][h][:]
             return raw_e[e][0][:, :, h * half : (h + 1) * half]
 
         g_w = sb([P, T], U32, "g_w")
@@ -168,11 +168,15 @@ def tile_moe_hib_relu_kernel(
         for first in (0, C1):
             nc.vector.tensor_copy(g_s0[:, first : first + C1], dy_s[:].indirect(entries(dst_t, first, C1)))
 
-        wins = {g: [sb([P, (g + 1) * C1], F32, "win%d_%d" % (g, r)) for r in range(PACK)] for g in range(GROUPS)}
+        wins = {
+            g: [sb([P, (g + 1) * C1], F32, "win%d_%d" % (g, r)) for r in range(PACK - (g == GROUPS - 1))]
+            for g in range(GROUPS)
+        }
         we = {0: expert_weights(0)}
         g_s1 = sb([P, C1], U8, "g_s1", tag="stage_first")
         nc.vector.tensor_copy(g_s1[:], dy_s[:].indirect(entries(dst_t, 2 * C1, C1)))
         banks = {}
+        zs = {}
 
         def first_products(e):
             slots = slice(e * C2, (e + 1) * C2)
@@ -181,22 +185,29 @@ def tile_moe_hib_relu_kernel(
             for r in range(PACK):
                 mm(banks[e][:, r, :], we[e], r, g_w[:, slots], scales)
 
-        def first_scatters(e, z):
+        def gated(e, z):
             g, x = divmod(e, 2)
+            zs[e] = z
             nc.vector.tensor_tensor(
                 out=z,
                 in0=banks[e][:],
                 in1=gates[g][:, x * C2 : (x + 1) * C2].unsqueeze(1).to_broadcast([P, PACK, C2]),
                 op=MULT,
             )
+
+        def scalar_scatters(e):
             for r in range(PACK):
-                engine = "vector" if (g, r) == (1, PACK - 1) else "scalar"
-                scatter_on(engine, wins[g][r], entries(offs2_t, e * C2, C2), z[:, r, :])
+                if (e // 2, r) != (GROUPS - 1, PACK - 1):
+                    scatter_on("vector" if (e, r) == (2, PACK - 1) else "scalar", wins[e // 2][r], entries(offs2_t, e * C2, C2), zs[e][:, r, :])
 
         for e in range(EXPERTS - 1):
             first_products(e)
+            if e == 0:
+                gated(e, sb([P, PACK, C2], F32, "z0")[:])
             we[e + 1] = expert_weights(e + 1)
-            first_scatters(e, sb([P, PACK, C2], F32, "z0")[:] if e == 0 else raw_half(e + 1, 0)[:, :, :C2])
+            if e > 0:
+                gated(e, raw_half(e + 1, 0)[:, :, :C2])
+            scalar_scatters(e)
         first_products(EXPERTS - 1)
 
         dx = {}
@@ -227,6 +238,14 @@ def tile_moe_hib_relu_kernel(
         outs.append(sb([P, T], F32, "out3"))
 
         def products(g, wg, da_q):
+            if g == GROUPS - 1:
+                for r in (0, 2, 1):
+                    banks[g, r] = psum.tile([P, C1], F32, name="bank", tag="bank%d" % (r + 2))
+                    mm(banks[g, r][:], wg, r, da_q[0][:], da_q[1][:])
+                dx[g, 0] = sb([P, C1], F32, "dx%d" % g)[:]
+                copy_on("scalar", dx[g, 0], banks[g, 0][:])
+                second_scatter("scalar", g, 0)
+                return
             for h in (1, 0):
                 banks[g, h] = psum.tile([P, 2, C1], F32, name="bank", tag="bank%d" % ((EXPERTS + 2 * g + h) % 8))
                 for r in range(2):
@@ -241,39 +260,48 @@ def tile_moe_hib_relu_kernel(
                 dx[g, 2 + r] = dest[:, r, :]
 
         for g in range(GROUPS):
-            planes = sb([P, PACK, C1], BF16, "planes%d" % g)
+            tag = "wgt%d" % (g - 1) if g else "planes0"
+            planes = sb([P, PACK, C1], BF16, "planes%d" % g, tag=tag)
             mask_planes(g, planes, range(PACK))
+            codes = sb([P, W], U32, "wg%d_codes" % g)
+            scales = sb([P, W], U8, "wg%d_scales" % g)
+            wg = (codes, scales)
+            own = sb([P, (W - LENT) * PACK], BF16, "stage_own%d" % g, tag="win%d_1" % g)
+            weave("vector", own[:], raw_own[g])
+            staged = sb([P, C1 * PACK], BF16, "stage_da%d" % g)
+            weave("vector", staged[:], planes[:])
+            nc.vector.quantize_mx(out=codes[:, LENT:].bitcast(FP8X4), scales=scales[:, LENT:], in_=own[:])
+            da_q = quantize(staged[:], C1, "da%d" % g)
+            lent = sb([P, LENT * PACK], BF16, "stage_lent%d" % g, tag="win%d_1" % g)
+            copy_on(
+                "gpsimd",
+                lent[:].rearrange("p (c j) -> p c j", j=PACK),
+                raw_lent[g].rearrange("p j c -> p c j"),
+            )
             if g == 0:
-                first_scatters(EXPERTS - 1, pre[g][:, 0:2, :].rearrange("p a (b c) -> p (a b) c", b=2))
-                staged = sb([P, C1 * PACK], BF16, "stage_da%d" % g)
-                weave("vector", staged[:], planes[:])
-                da_q = quantize(staged[:], C1, "da%d" % g)
-                staged = sb([P, W * PACK], BF16, "stage_g%d" % g, tag="win%d_3" % g)
-                weave("vector", staged[:], raw_g[g][:])
-                wg = quantize(staged[:], W, "wg%d" % g)
+                gated(EXPERTS - 1, sb([P, PACK, C2], F32, "z_last", tag="planes0")[:])
+                wins[2].append(sb([P, T], F32, "win_held", tag="stage_da0"))
+                for e in (4, 5):
+                    scatter_on("vector", wins[2][3], entries(offs2_t, e * C2, C2), zs[e][:, 3, :])
+                scalar_scatters(EXPERTS - 1)
             else:
-                codes = sb([P, W], U32, "wg%d_codes" % g)
-                scales = sb([P, W], U8, "wg%d_scales" % g)
-                wg = (codes, scales)
-                own = sb([P, OWN * PACK], BF16, "stage_own%d" % g, tag="win%d_1" % g)
-                weave("vector", own[:], raw_g[g][:, :, :OWN])
-                staged = sb([P, C1 * PACK], BF16, "stage_da%d" % g)
-                weave("vector", staged[:], planes[:])
-                nc.vector.quantize_mx(out=codes[:, :OWN].bitcast(FP8X4), scales=scales[:, :OWN], in_=own[:])
-                da_q = quantize(staged[:], C1, "da%d" % g)
-                lent = sb([P, (W - OWN) * PACK], BF16, "stage_lent%d" % g, tag="stage_da%d" % g)
-                copy_on(
-                    "gpsimd",
-                    lent[:].rearrange("p (c j) -> p c j", j=PACK),
-                    raw_g[g][:, :, OWN:].rearrange("p j c -> p c j"),
-                )
-                empty_high(g - 1, sb([P, 2, C1], F32, "dx_high%d" % g, tag="planes%d" % g)[:])
+                empty_high(g - 1, sb([P, 2, C1], F32, "dx_high%d" % g, tag=tag)[:])
                 second_scatter("vector", g - 1, 3)
                 second_scatter("scalar", g - 1, 2)
-                nc.vector.quantize_mx(out=codes[:, OWN:].bitcast(FP8X4), scales=scales[:, OWN:], in_=lent[:])
+            if g == GROUPS - 1:
+                banks[g, 3] = psum.tile([P, C1], F32, name="bank", tag="bank5")
+                mm(banks[g, 3][:], wg, 3, da_q[0][:], da_q[1][:])
+                dx[g, 3] = sb([P, C1], F32, "dx_own", tag="wgt2")[:]
+                copy_on("vector", dx[g, 3], banks[g, 3][:])
+            nc.vector.quantize_mx(out=codes[:, :LENT].bitcast(FP8X4), scales=scales[:, :LENT], in_=lent[:])
+            if g == GROUPS - 1:
+                second_scatter("vector", g, 3)
             products(g, wg, da_q)
-        empty_high(2, sb([P, 2, C1], F32, "dx_last")[:])
-        for r in (3, 2):
-            second_scatter("vector", 2, r)
+        last = sb([P, 2, C1], F32, "dx_last")
+        for r in (2, 1):
+            copy_on("vector", last[:, r - 1, :], banks[2, r][:])
+            dx[2, r] = last[:, r - 1, :]
+        second_scatter("vector", 2, 2)
+        second_scatter("scalar", 2, 1)
         for r in (3, 0, 2, 1):
             nc.sync.dma_start(out=out[r * P : (r + 1) * P, :], in_=outs[r][:])

@@ -1,6 +1,7 @@
 from contextlib import ExitStack
 
 import concourse.mybir as mybir
+from concourse.masks import make_identity
 
 F32 = mybir.dt.float32
 BF16 = mybir.dt.bfloat16
@@ -24,7 +25,7 @@ C2 = 128
 EXPERTS = 6
 PER_COL = 16
 LENT = 384
-SCALAR_WORDS = 44
+SCALAR_WORDS = (44, 52)
 
 FLOPS = 2 * 2 * W * W * T
 
@@ -36,6 +37,7 @@ def tile_moe_hib_relu_kernel(
     with ExitStack() as ctx:
         lists = ctx.enter_context(tc.tile_pool(name="lists", bufs=1))
         keep = ctx.enter_context(tc.tile_pool(name="keep", bufs=1))
+        placed = ctx.enter_context(tc.tile_pool(name="placed", bufs=1))
         psum = ctx.enter_context(tc.psum_pool(name="psum", bufs=1))
 
         def sb(shape, dtype, name, tag=None):
@@ -56,10 +58,21 @@ def tile_moe_hib_relu_kernel(
             )
             return tile
 
-        def load_gate(g):
-            tile = sb([P, C1], F32, "gate%d" % g)
-            nc.sync.dma_start(out=tile[:], in_=gate[:, g * C1 : (g + 1) * C1])
+        def load_gate(first, each, name):
+            tile = sb([P, each], F32, name)
+            nc.sync.dma_start(
+                out=tile[:], in_=gate[0, first : first + P * each].rearrange("(q c) -> q c", c=each)
+            )
             return tile
+
+        def spread_gate(column, first, each, tag):
+            bank = psum.tile([P, each, P], F32, name="bank", tag=tag)
+            for c in range(each):
+                nc.tensor.transpose(bank[:, c, :], column[:, c : c + 1].to_broadcast([P, P]), ident[:])
+            nc.scalar.copy(
+                out=gates[:, first : first + P * each].rearrange("p (q c) -> p q c", c=each),
+                in_=bank[:].rearrange("p c q -> p q c"),
+            )
 
         def copy_on(engine, out_ap, in_ap):
             if engine == "vector":
@@ -111,23 +124,24 @@ def tile_moe_hib_relu_kernel(
                 out=dy_s[:].bitcast(I32)[32 * q : 32 * (q + 1), :],
                 in_=scale_rows[PACK * q : PACK * (q + 1), :].unsqueeze(0).to_broadcast([8, PACK, T // 4]),
             )
+        ident = sb([P, P], F32, "ident")
+        make_identity(nc, ident[:])
+        gates = sb([P, T], F32, "gates")
+        spread_gate(load_gate(0, 4, "column4"), 0, 4, "bank6")
         nc.sync.dma_start(
             out=dy_w[:].bitcast(I32), in_=dy_words[0].rearrange("p t d -> p (t d)").bitcast(I32)
         )
         raw_e = {}
-        gates = {}
         pre = {}
         raw_g = {}
         raw_e[0] = [load_rows(wet[0], 0, W, "wet0")]
-        gates[0] = load_gate(0)
+        spread_gate(load_gate(4 * P, 2, "column2"), 4 * P, 2, "bank7")
         offs2_t = load_list(offs2, "offs2_t")
         raw_e[1] = [load_rows(wet[1], 0, W, "wet1")]
         raw_e[2] = [load_rows(wet[2], 0, W, "wet2")]
         raw_e[3] = [load_rows(wet[3], 0, W, "wet3")]
-        gates[1] = load_gate(1)
         raw_e[4] = [load_rows(wet[4], 0, W, "wet4")]
         raw_e[5] = [load_rows(wet[5], 0, W, "wet5")]
-        gates[2] = load_gate(2)
         pre[0] = load_rows(a, 0, C1, "a0")
         raw_own = {0: load_rows(wgt[0], LENT, W - LENT, "wgt0_own")[:]}
         offs_t = load_list(offs, "offs_t")
@@ -146,9 +160,12 @@ def tile_moe_hib_relu_kernel(
             return ring[len(taken) % 2][:, :width]
 
         def expert_weights(e):
-            staged = sb([P, W * PACK], BF16, "stage_first")[:] if e == 0 else stage(W * PACK)
+            if e < 2:
+                staged = placed.tile([P, W * PACK], BF16, name="stage_e%d" % e, offset=e * C1, align_bytes=64)[:]
+            else:
+                staged = stage(W * PACK)
             view = staged.rearrange("p (t m j) -> p m j t", t=PACK, j=PACK)
-            cut = SCALAR_WORDS if e < 2 else P // 2
+            cut = SCALAR_WORDS[e] if e < 2 else P // 2
             for h, (first, last) in enumerate(((0, cut), (cut, P))):
                 rows = raw_e[e][0][:, :, PACK * first : PACK * last]
                 copy_on(
@@ -173,7 +190,7 @@ def tile_moe_hib_relu_kernel(
             for g in range(GROUPS)
         }
         we = {0: expert_weights(0)}
-        g_s1 = sb([P, C1], U8, "g_s1", tag="stage_first")
+        g_s1 = placed.tile([P, C1], U8, name="g_s1", offset=0, align_bytes=64)
         nc.vector.tensor_copy(g_s1[:], dy_s[:].indirect(entries(dst_t, 2 * C1, C1)))
         banks = {}
         zs = {}
@@ -186,12 +203,11 @@ def tile_moe_hib_relu_kernel(
                 mm(banks[e][:, r, :], we[e], r, g_w[:, slots], scales)
 
         def gated(e, z):
-            g, x = divmod(e, 2)
             zs[e] = z
             nc.vector.tensor_tensor(
                 out=z,
                 in0=banks[e][:],
-                in1=gates[g][:, x * C2 : (x + 1) * C2].unsqueeze(1).to_broadcast([P, PACK, C2]),
+                in1=gates[:, e * C2 : (e + 1) * C2].unsqueeze(1).to_broadcast([P, PACK, C2]),
                 op=MULT,
             )
 

@@ -262,7 +262,7 @@ def tile_moe_hib_relu_kernel(
                 copy_on("scalar", dx[g, 0], banks[g, 0][:])
                 second_scatter("scalar", g, 0)
                 return
-            for h in (1, 0):
+            for h in range(2):
                 banks[g, h] = psum.tile([P, 2, C1], F32, name="bank", tag="bank%d" % ((EXPERTS + 2 * g + h) % 8))
                 for r in range(2):
                     mm(banks[g, h][:, r, :], wg, 2 * h + r, da_q[0][:], da_q[1][:])

@@ -126,8 +126,6 @@ def tile_moe_hib_relu_kernel(
             )
         ident = sb([P, P], F32, "ident")
         make_identity(nc, ident[:])
-        gates = sb([P, T], F32, "gates")
-        spread_gate(load_gate(0, 4, "column4"), 0, 4, "bank6")
         nc.sync.dma_start(
             out=dy_w[:].bitcast(I32), in_=dy_words[0].rearrange("p t d -> p (t d)").bitcast(I32)
         )
@@ -135,9 +133,9 @@ def tile_moe_hib_relu_kernel(
         pre = {}
         raw_g = {}
         raw_e[0] = [load_rows(wet[0], 0, W, "wet0")]
-        spread_gate(load_gate(4 * P, 2, "column2"), 4 * P, 2, "bank7")
-        offs2_t = load_list(offs2, "offs2_t")
+        columns = [load_gate(0, 4, "column4"), load_gate(4 * P, 2, "column2")]
         raw_e[1] = [load_rows(wet[1], 0, W, "wet1")]
+        offs2_t = load_list(offs2, "offs2_t")
         raw_e[2] = [load_rows(wet[2], 0, W, "wet2")]
         raw_e[3] = [load_rows(wet[3], 0, W, "wet3")]
         raw_e[4] = [load_rows(wet[4], 0, W, "wet4")]
@@ -190,6 +188,9 @@ def tile_moe_hib_relu_kernel(
             for g in range(GROUPS)
         }
         we = {0: expert_weights(0)}
+        gates = sb([P, T], F32, "gates", tag="wet0")
+        spread_gate(columns[0], 0, 4, "bank6")
+        spread_gate(columns[1], 4 * P, 2, "bank7")
         g_s1 = placed.tile([P, C1], U8, name="g_s1", offset=0, align_bytes=64)
         nc.vector.tensor_copy(g_s1[:], dy_s[:].indirect(entries(dst_t, 2 * C1, C1)))
         banks = {}
@@ -197,24 +198,33 @@ def tile_moe_hib_relu_kernel(
 
         def first_products(e):
             slots = slice(e * C2, (e + 1) * C2)
-            banks[e] = psum.tile([P, PACK, C2], F32, name="bank", tag="bank%d" % e)
             scales = g_s0[:, slots] if e < 4 else g_s1[:, (e - 4) * C2 : (e - 3) * C2]
-            for r in range(PACK):
-                mm(banks[e][:, r, :], we[e], r, g_w[:, slots], scales)
+            cuts = (0, 1, PACK) if e == 0 else (0, PACK)
+            banks[e] = []
+            for first, last in zip(cuts, cuts[1:]):
+                tag = "bank%d" % (e if last == PACK else EXPERTS - 1)
+                bank = psum.tile([P, last - first, C2], F32, name="bank", tag=tag)
+                banks[e].append((first, last, bank))
+                for r in range(first, last):
+                    mm(bank[:, r - first, :], we[e], r, g_w[:, slots], scales)
 
         def gated(e, z):
             zs[e] = z
-            nc.vector.tensor_tensor(
-                out=z,
-                in0=banks[e][:],
-                in1=gates[:, e * C2 : (e + 1) * C2].unsqueeze(1).to_broadcast([P, PACK, C2]),
-                op=MULT,
-            )
+            for first, last, bank in banks[e]:
+                nc.vector.tensor_tensor(
+                    out=z[:, first:last, :],
+                    in0=bank[:],
+                    in1=gates[:, e * C2 : (e + 1) * C2].unsqueeze(1).to_broadcast([P, last - first, C2]),
+                    op=MULT,
+                )
 
         def scalar_scatters(e):
             for r in range(PACK):
-                if (e // 2, r) != (GROUPS - 1, PACK - 1):
-                    scatter_on("vector" if (e, r) == (2, PACK - 1) else "scalar", wins[e // 2][r], entries(offs2_t, e * C2, C2), zs[e][:, r, :])
+                if (e, r) == (2, PACK - 1):
+                    for engine, first in (("vector", 0), ("scalar", C2 // 2)):
+                        scatter_on(engine, wins[1][r], entries(offs2_t, e * C2 + first, C2 // 2), zs[e][:, r, first : first + C2 // 2])
+                elif (e // 2, r) != (GROUPS - 1, PACK - 1):
+                    scatter_on("scalar", wins[e // 2][r], entries(offs2_t, e * C2, C2), zs[e][:, r, :])
 
         for e in range(EXPERTS - 1):
             first_products(e)
@@ -254,14 +264,6 @@ def tile_moe_hib_relu_kernel(
         outs.append(sb([P, T], F32, "out3"))
 
         def products(g, wg, da_q):
-            if g == GROUPS - 1:
-                for r in (0, 2, 1):
-                    banks[g, r] = psum.tile([P, C1], F32, name="bank", tag="bank%d" % (r + 2))
-                    mm(banks[g, r][:], wg, r, da_q[0][:], da_q[1][:])
-                dx[g, 0] = sb([P, C1], F32, "dx%d" % g)[:]
-                copy_on("scalar", dx[g, 0], banks[g, 0][:])
-                second_scatter("scalar", g, 0)
-                return
             for h in range(2):
                 banks[g, h] = psum.tile([P, 2, C1], F32, name="bank", tag="bank%d" % ((EXPERTS + 2 * g + h) % 8))
                 for r in range(2):
@@ -305,19 +307,38 @@ def tile_moe_hib_relu_kernel(
                 second_scatter("vector", g - 1, 3)
                 second_scatter("scalar", g - 1, 2)
             if g == GROUPS - 1:
-                banks[g, 3] = psum.tile([P, C1], F32, name="bank", tag="bank5")
-                mm(banks[g, 3][:], wg, 3, da_q[0][:], da_q[1][:])
-                dx[g, 3] = sb([P, C1], F32, "dx_own", tag="wgt2")[:]
-                copy_on("vector", dx[g, 3], banks[g, 3][:])
-            nc.vector.quantize_mx(out=codes[:, :LENT].bitcast(FP8X4), scales=scales[:, :LENT], in_=lent[:])
-            if g == GROUPS - 1:
-                second_scatter("vector", g, 3)
-            products(g, wg, da_q)
-        last = sb([P, 2, C1], F32, "dx_last")
+                early = psum.tile([P, C2], F32, name="bank", tag="bank5")
+                mm(early[:], wg, 3, da_q[0][:, :C2], da_q[1][:, :C2])
+                dx_early = sb([P, C2], F32, "dx_own", tag="wgt2")
+                copy_on("vector", dx_early[:], early[:])
+            cuts = (0, P, LENT) if g == GROUPS - 1 else (0, LENT)
+            for first, last in zip(cuts, cuts[1:]):
+                nc.vector.quantize_mx(
+                    out=codes[:, first:last].bitcast(FP8X4),
+                    scales=scales[:, first:last],
+                    in_=lent[:, first * PACK : last * PACK],
+                )
+            if g < GROUPS - 1:
+                products(g, wg, da_q)
+        g = GROUPS - 1
+        scatter_on("vector", outs[3], entries(offs_t, g * C1, C2), dx_early[:])
+        mixed = psum.tile([P, C1 + C2], F32, name="bank", tag="bank2")
+        mm(mixed[:, :C1], wg, 0, da_q[0][:], da_q[1][:])
+        mm(mixed[:, C1:], wg, 3, da_q[0][:, C2:], da_q[1][:, C2:])
         for r in (2, 1):
-            copy_on("vector", last[:, r - 1, :], banks[2, r][:])
-            dx[2, r] = last[:, r - 1, :]
-        second_scatter("vector", 2, 2)
-        second_scatter("scalar", 2, 1)
+            banks[g, r] = psum.tile([P, C1], F32, name="bank", tag="bank%d" % (r + 2))
+            mm(banks[g, r][:], wg, r, da_q[0][:], da_q[1][:])
+        dx_mixed = sb([P, C1 + C2], F32, "dx_mixed")
+        copy_on("vector", dx_mixed[:], mixed[:])
+        dx[g, 0] = dx_mixed[:, :C1]
+        second_scatter("scalar", g, 0)
+        dx_pair = sb([P, 2, C1], F32, "dx_pair")
+        for r in (2, 1):
+            dx[g, r] = dx_pair[:, r - 1, :]
+            copy_on("vector", dx[g, r], banks[g, r][:])
+            if r == 2:
+                scatter_on("vector", outs[3], entries(offs_t, g * C1 + C2, C2), dx_mixed[:, C1:])
+        second_scatter("vector", g, 2)
+        second_scatter("scalar", g, 1)
         for r in (3, 0, 2, 1):
             nc.sync.dma_start(out=out[r * P : (r + 1) * P, :], in_=outs[r][:])

@@ -24,7 +24,9 @@ C1 = 256
 C2 = 128
 EXPERTS = 6
 PER_COL = 16
-LENT = 384
+LENT = 336
+LATE = 384
+OVERLAP = 32
 SCALAR_WORDS = (44, 52)
 
 FLOPS = 2 * 2 * W * W * T
@@ -284,16 +286,18 @@ def tile_moe_hib_relu_kernel(
             codes = sb([P, W], U32, "wg%d_codes" % g)
             scales = sb([P, W], U8, "wg%d_scales" % g)
             wg = (codes, scales)
-            own = sb([P, (W - LENT) * PACK], BF16, "stage_own%d" % g, tag="win%d_1" % g)
-            weave("vector", own[:], raw_own[g])
+            staging = sb([P, W * PACK - OVERLAP], BF16, "stage_g%d" % g, tag="win%d_1" % g)
+            own = staging[:, : (W - LATE) * PACK]
+            late = staging[:, (W - LATE) * PACK - OVERLAP :]
+            weave("vector", own, raw_own[g][:, :, LATE - LENT :])
+            weave("vector", late[:, LENT * PACK :], raw_own[g][:, :, : LATE - LENT])
             staged = sb([P, C1 * PACK], BF16, "stage_da%d" % g)
             weave("vector", staged[:], planes[:])
-            nc.vector.quantize_mx(out=codes[:, LENT:].bitcast(FP8X4), scales=scales[:, LENT:], in_=own[:])
+            nc.vector.quantize_mx(out=codes[:, LATE:].bitcast(FP8X4), scales=scales[:, LATE:], in_=own)
             da_q = quantize(staged[:], C1, "da%d" % g)
-            lent = sb([P, LENT * PACK], BF16, "stage_lent%d" % g, tag="win%d_1" % g)
             copy_on(
                 "gpsimd",
-                lent[:].rearrange("p (c j) -> p c j", j=PACK),
+                late[:, : LENT * PACK].rearrange("p (c j) -> p c j", j=PACK),
                 raw_lent[g].rearrange("p j c -> p c j"),
             )
             if g == 0:
@@ -311,12 +315,12 @@ def tile_moe_hib_relu_kernel(
                 mm(early[:], wg, 3, da_q[0][:, :C2], da_q[1][:, :C2])
                 dx_early = sb([P, C2], F32, "dx_own", tag="wgt2")
                 copy_on("vector", dx_early[:], early[:])
-            cuts = (0, P, LENT) if g == GROUPS - 1 else (0, LENT)
+            cuts = (0, P, LATE) if g == GROUPS - 1 else (0, LATE)
             for first, last in zip(cuts, cuts[1:]):
                 nc.vector.quantize_mx(
                     out=codes[:, first:last].bitcast(FP8X4),
                     scales=scales[:, first:last],
-                    in_=lent[:, first * PACK : last * PACK],
+                    in_=late[:, first * PACK : last * PACK],
                 )
             if g < GROUPS - 1:
                 products(g, wg, da_q)

@@ -222,10 +222,7 @@ def tile_moe_hib_relu_kernel(
 
         def scalar_scatters(e):
             for r in range(PACK):
-                if (e, r) == (2, PACK - 1):
-                    for engine, first in (("vector", 0), ("scalar", C2 // 2)):
-                        scatter_on(engine, wins[1][r], entries(offs2_t, e * C2 + first, C2 // 2), zs[e][:, r, first : first + C2 // 2])
-                elif (e // 2, r) != (GROUPS - 1, PACK - 1):
+                if (e // 2, r) != (GROUPS - 1, PACK - 1):
                     scatter_on("scalar", wins[e // 2][r], entries(offs2_t, e * C2, C2), zs[e][:, r, :])
 
         for e in range(EXPERTS - 1):

from contextlib import ExitStack

import concourse.mybir as mybir
from concourse.masks import make_identity

F32 = mybir.dt.float32
BF16 = mybir.dt.bfloat16
I32 = mybir.dt.int32
U32 = mybir.dt.uint32
U16 = mybir.dt.uint16
U8 = mybir.dt.uint8
FP8X4 = mybir.dt.float8_e4m3fn_x4
MULT = mybir.AluOpType.mult
ADD = mybir.AluOpType.add
IS_GT = mybir.AluOpType.is_gt
COPY = mybir.ActivationFunctionType.Copy

P = 128
PACK = 4
W = 512
T = 768
GROUPS = 3
C1 = 256
C2 = 128
EXPERTS = 6
PER_COL = 16
LENT = 336
LATE = 384
OVERLAP = 32
SCALAR_WORDS = (44, 52)

FLOPS = 2 * 2 * W * W * T


def tile_moe_hib_relu_kernel(
    tc, dy_words, dy_scales, wet, wgt, a, gate, offs, offs2, dst, out
):
    nc = tc.nc
    with ExitStack() as ctx:
        lists = ctx.enter_context(tc.tile_pool(name="lists", bufs=1))
        keep = ctx.enter_context(tc.tile_pool(name="keep", bufs=1))
        placed = ctx.enter_context(tc.tile_pool(name="placed", bufs=1))
        psum = ctx.enter_context(tc.psum_pool(name="psum", bufs=1))

        def sb(shape, dtype, name, tag=None):
            return keep.tile(shape, dtype, name=name, tag=tag or name, align_bytes=64)

        def load_list(src, name):
            tile = lists.tile([P, T // PER_COL], U16, name=name)
            nc.sync.dma_start(tile[:], src)
            return tile

        def entries(tile, first, count):
            return tile[:, first // PER_COL : (first + count) // PER_COL]

        def load_rows(src, first, count, name):
            tile = sb([P, PACK, count], F32, name)
            nc.sync.dma_start(
                out=tile[:], in_=src.rearrange("(p j) c -> p j c", j=PACK)[:, :, first : first + count]
            )
            return tile

        def load_gate(first, each, name):
            tile = sb([P, each], F32, name)
            nc.sync.dma_start(
                out=tile[:], in_=gate[0, first : first + P * each].rearrange("(q c) -> q c", c=each)
            )
            return tile

        def spread_gate(column, first, each, tag):
            bank = psum.tile([P, each, P], F32, name="bank", tag=tag)
            for c in range(each):
                nc.tensor.transpose(bank[:, c, :], column[:, c : c + 1].to_broadcast([P, P]), ident[:])
            nc.scalar.copy(
                out=gates[:, first : first + P * each].rearrange("p (q c) -> p q c", c=each),
                in_=bank[:].rearrange("p c q -> p q c"),
            )

        def copy_on(engine, out_ap, in_ap):
            if engine == "vector":
                nc.vector.tensor_copy(out=out_ap, in_=in_ap)
            elif engine == "gpsimd":
                nc.gpsimd.tensor_scalar(out=out_ap, in0=in_ap, scalar1=1.0, scalar2=0.0, op0=MULT, op1=ADD)
            else:
                nc.scalar.copy(out=out_ap, in_=in_ap)

        def scatter_on(engine, window, offsets, values):
            if engine == "vector":
                nc.vector.tensor_copy(window[:].indirect(offsets), values)
            else:
                nc.scalar.activation(window[:].indirect(offsets), values, COPY)

        def weave(engine, staged, rows):
            copy_on(
                engine,
                staged.rearrange("p (c i j) -> p c j i", i=PACK, j=PACK),
                rows.rearrange("p j (c i) -> p c j i", i=PACK),
            )

        def quantize(staged, words, name):
            codes = sb([P, words], U32, name + "_codes")
            scales = sb([P, words], U8, name + "_scales")
            nc.vector.quantize_mx(out=codes[:].bitcast(FP8X4), scales=scales[:], in_=staged)
            return codes, scales

        def mm(acc, w, col, x_codes, x_scales):
            cols = slice(col * P, (col + 1) * P)
            nc.tensor.matmul_mx(
                out=acc,
                lhsT=w[0][:, cols].bitcast(FP8X4),
                lhsT_scale=w[1][:, cols],
                rhs=x_codes.bitcast(FP8X4),
                rhs_scale=x_scales,
                start=True,
                stop=True,
            )

        half = W // 2

        dy_w = sb([P, T], U32, "dy_w")
        dy_s = sb([P, T], U8, "dy_s")
        dst_t = load_list(dst, "dst_t")
        scale_rows = dy_scales[0].bitcast(I32)
        for q in range(PACK):
            nc.sync.dma_start(
                out=dy_s[:].bitcast(I32)[32 * q : 32 * (q + 1), :],
                in_=scale_rows[PACK * q : PACK * (q + 1), :].unsqueeze(0).to_broadcast([8, PACK, T // 4]),
            )
        ident = sb([P, P], F32, "ident")
        make_identity(nc, ident[:])
        nc.sync.dma_start(
            out=dy_w[:].bitcast(I32), in_=dy_words[0].rearrange("p t d -> p (t d)").bitcast(I32)
        )
        raw_e = {}
        pre = {}
        raw_g = {}
        raw_e[0] = [load_rows(wet[0], 0, W, "wet0")]
        columns = [load_gate(0, 4, "column4"), load_gate(4 * P, 2, "column2")]
        raw_e[1] = [load_rows(wet[1], 0, W, "wet1")]
        offs2_t = load_list(offs2, "offs2_t")
        raw_e[2] = [load_rows(wet[2], 0, W, "wet2")]
        raw_e[3] = [load_rows(wet[3], 0, W, "wet3")]
        raw_e[4] = [load_rows(wet[4], 0, W, "wet4")]
        raw_e[5] = [load_rows(wet[5], 0, W, "wet5")]
        pre[0] = load_rows(a, 0, C1, "a0")
        raw_own = {0: load_rows(wgt[0], LENT, W - LENT, "wgt0_own")[:]}
        offs_t = load_list(offs, "offs_t")
        raw_lent = {0: load_rows(wgt[0], 0, LENT, "wgt0")[:]}
        for g in range(1, GROUPS):
            raw_g[g] = load_rows(wgt[g], 0, W, "wgt%d" % g)
            raw_own[g] = raw_g[g][:, :, LENT:]
            raw_lent[g] = raw_g[g][:, :, :LENT]
            pre[g] = load_rows(a, g * C1, C1, "a%d" % g)

        ring = [sb([P, W * PACK], BF16, "stage%d" % s) for s in range(2)]
        taken = []

        def stage(width):
            taken.append(width)
            return ring[len(taken) % 2][:, :width]

        def expert_weights(e):
            if e < 2:
                staged = placed.tile([P, W * PACK], BF16, name="stage_e%d" % e, offset=e * C1, align_bytes=64)[:]
            else:
                staged = stage(W * PACK)
            view = staged.rearrange("p (t m j) -> p m j t", t=PACK, j=PACK)
            cut = SCALAR_WORDS[e] if e < 2 else P // 2
            for h, (first, last) in enumerate(((0, cut), (cut, P))):
                rows = raw_e[e][0][:, :, PACK * first : PACK * last]
                copy_on(
                    "scalar" if (e < 2 and h == 0) else "vector",
                    view[:, first:last],
                    rows.rearrange("p j (m t) -> p m j t", t=PACK),
                )
            return quantize(staged, W, "we%d" % e)

        def raw_half(e, h):
            return raw_e[e][0][:, :, h * half : (h + 1) * half]

        g_w = sb([P, T], U32, "g_w")
        for first, count in ((0, C1), (C1, T - C1)):
            nc.vector.tensor_copy(g_w[:, first : first + count], dy_w[:].indirect(entries(dst_t, first, count)))
        g_s0 = sb([P, 2 * C1], U8, "g_s0")
        for first in (0, C1):
            nc.vector.tensor_copy(g_s0[:, first : first + C1], dy_s[:].indirect(entries(dst_t, first, C1)))

        wins = {
            g: [sb([P, (g + 1) * C1], F32, "win%d_%d" % (g, r)) for r in range(PACK - (g == GROUPS - 1))]
            for g in range(GROUPS)
        }
        we = {0: expert_weights(0)}
        gates = sb([P, T], F32, "gates", tag="wet0")
        spread_gate(columns[0], 0, 4, "bank6")
        spread_gate(columns[1], 4 * P, 2, "bank7")
        g_s1 = placed.tile([P, C1], U8, name="g_s1", offset=0, align_bytes=64)
        nc.vector.tensor_copy(g_s1[:], dy_s[:].indirect(entries(dst_t, 2 * C1, C1)))
        banks = {}
        zs = {}

        def first_products(e):
            slots = slice(e * C2, (e + 1) * C2)
            scales = g_s0[:, slots] if e < 4 else g_s1[:, (e - 4) * C2 : (e - 3) * C2]
            cuts = (0, 1, PACK) if e == 0 else (0, PACK)
            banks[e] = []
            for first, last in zip(cuts, cuts[1:]):
                tag = "bank%d" % (e if last == PACK else EXPERTS - 1)
                bank = psum.tile([P, last - first, C2], F32, name="bank", tag=tag)
                banks[e].append((first, last, bank))
                for r in range(first, last):
                    mm(bank[:, r - first, :], we[e], r, g_w[:, slots], scales)

        def gated(e, z):
            zs[e] = z
            for first, last, bank in banks[e]:
                nc.vector.tensor_tensor(
                    out=z[:, first:last, :],
                    in0=bank[:],
                    in1=gates[:, e * C2 : (e + 1) * C2].unsqueeze(1).to_broadcast([P, last - first, C2]),
                    op=MULT,
                )

        def scalar_scatters(e):
            for r in range(PACK):
                if (e // 2, r) != (GROUPS - 1, PACK - 1):
                    scatter_on("scalar", wins[e // 2][r], entries(offs2_t, e * C2, C2), zs[e][:, r, :])

        for e in range(EXPERTS - 1):
            first_products(e)
            if e == 0:
                gated(e, sb([P, PACK, C2], F32, "z0")[:])
            we[e + 1] = expert_weights(e + 1)
            if e > 0:
                gated(e, raw_half(e + 1, 0)[:, :, :C2])
            scalar_scatters(e)
        first_products(EXPERTS - 1)

        dx = {}
        outs = [sb([P, T], F32, "out%d" % r) for r in range(PACK - 1)]

        def mask_planes(g, planes, rows):
            for r in rows:
                nc.vector.scalar_tensor_tensor(
                    out=planes[:, r, :],
                    in0=pre[g][:, r, :],
                    scalar=0.0,
                    in1=wins[g][r][:, g * C1 : (g + 1) * C1],
                    op0=IS_GT,
                    op1=MULT,
                )

        def empty(engine, g, h, dest):
            if engine == "vector":
                copy_on(engine, dest, banks[g, h][:])
            for r in range(2):
                if engine == "scalar":
                    copy_on(engine, dest[:, r, :], banks[g, h][:, r, :])
                dx[g, 2 * h + r] = dest[:, r, :]

        def second_scatter(engine, g, r, first=0, count=C1):
            scatter_on(engine, outs[r], entries(offs_t, g * C1 + first, count), dx[g, r][:, first : first + count])

        outs.append(sb([P, T], F32, "out3"))

        def products(g, wg, da_q):
            for h in range(2):
                banks[g, h] = psum.tile([P, 2, C1], F32, name="bank", tag="bank%d" % ((EXPERTS + 2 * g + h) % 8))
                for r in range(2):
                    mm(banks[g, h][:, r, :], wg, 2 * h + r, da_q[0][:], da_q[1][:])
            empty("scalar", g, 0, sb([P, 2, C1], F32, "dx%d" % g)[:])
            for r in range(2):
                second_scatter("scalar", g, r)

        def empty_high(g, dest):
            for r in (1, 0):
                copy_on("vector", dest[:, r, :], banks[g, 1][:, r, :])
                dx[g, 2 + r] = dest[:, r, :]

        for g in range(GROUPS):
            tag = "wgt%d" % (g - 1) if g else "planes0"
            planes = sb([P, PACK, C1], BF16, "planes%d" % g, tag=tag)
            mask_planes(g, planes, range(PACK))
            codes = sb([P, W], U32, "wg%d_codes" % g)
            scales = sb([P, W], U8, "wg%d_scales" % g)
            wg = (codes, scales)
            staging = sb([P, W * PACK - OVERLAP], BF16, "stage_g%d" % g, tag="win%d_1" % g)
            own = staging[:, : (W - LATE) * PACK]
            late = staging[:, (W - LATE) * PACK - OVERLAP :]
            weave("vector", own, raw_own[g][:, :, LATE - LENT :])
            weave("vector", late[:, LENT * PACK :], raw_own[g][:, :, : LATE - LENT])
            staged = sb([P, C1 * PACK], BF16, "stage_da%d" % g)
            weave("vector", staged[:], planes[:])
            nc.vector.quantize_mx(out=codes[:, LATE:].bitcast(FP8X4), scales=scales[:, LATE:], in_=own)
            da_q = quantize(staged[:], C1, "da%d" % g)
            copy_on(
                "gpsimd",
                late[:, : LENT * PACK].rearrange("p (c j) -> p c j", j=PACK),
                raw_lent[g].rearrange("p j c -> p c j"),
            )
            if g == 0:
                gated(EXPERTS - 1, sb([P, PACK, C2], F32, "z_last", tag="planes0")[:])
                wins[2].append(sb([P, T], F32, "win_held", tag="stage_da0"))
                for e in (4, 5):
                    scatter_on("vector", wins[2][3], entries(offs2_t, e * C2, C2), zs[e][:, 3, :])
                scalar_scatters(EXPERTS - 1)
            else:
                empty_high(g - 1, sb([P, 2, C1], F32, "dx_high%d" % g, tag=tag)[:])
                second_scatter("vector", g - 1, 3)
                second_scatter("scalar", g - 1, 2)
            if g == GROUPS - 1:
                early = psum.tile([P, C2], F32, name="bank", tag="bank5")
                mm(early[:], wg, 3, da_q[0][:, :C2], da_q[1][:, :C2])
                dx_early = sb([P, C2], F32, "dx_own", tag="wgt2")
                copy_on("vector", dx_early[:], early[:])
            cuts = (0, P, LATE) if g == GROUPS - 1 else (0, LATE)
            for first, last in zip(cuts, cuts[1:]):
                nc.vector.quantize_mx(
                    out=codes[:, first:last].bitcast(FP8X4),
                    scales=scales[:, first:last],
                    in_=late[:, first * PACK : last * PACK],
                )
            if g < GROUPS - 1:
                products(g, wg, da_q)
        g = GROUPS - 1
        scatter_on("vector", outs[3], entries(offs_t, g * C1, C2), dx_early[:])
        mixed = psum.tile([P, C1 + C2], F32, name="bank", tag="bank2")
        mm(mixed[:, :C1], wg, 0, da_q[0][:], da_q[1][:])
        mm(mixed[:, C1:], wg, 3, da_q[0][:, C2:], da_q[1][:, C2:])
        for r in (2, 1):
            banks[g, r] = psum.tile([P, C1], F32, name="bank", tag="bank%d" % (r + 2))
            mm(banks[g, r][:], wg, r, da_q[0][:], da_q[1][:])
        dx_mixed = sb([P, C1 + C2], F32, "dx_mixed")
        copy_on("vector", dx_mixed[:], mixed[:])
        dx[g, 0] = dx_mixed[:, :C1]
        second_scatter("scalar", g, 0)
        dx_pair = sb([P, 2, C1], F32, "dx_pair")
        for r in (2, 1):
            dx[g, r] = dx_pair[:, r - 1, :]
            copy_on("vector", dx[g, r], banks[g, r][:])
            if r == 2:
                scatter_on("vector", outs[3], entries(offs_t, g * C1 + C2, C2), dx_mixed[:, C1:])
        second_scatter("vector", g, 2)
        second_scatter("scalar", g, 1)
        for r in (3, 0, 2, 1):
            nc.sync.dma_start(out=out[r * P : (r + 1) * P, :], in_=outs[r][:])
